import numpy as np, ml_dtypes
CORES = [23,119,17,113]
N = 4
BF = ml_dtypes.bfloat16
def gentries(a):
    return np.ascontiguousarray(a.reshape(8, 16, -1).transpose(0, 2, 1)).reshape(8, -1)
def gtable(e):
    e = np.asarray(e); return np.ascontiguousarray(e.reshape(8, -1, 16).transpose(0, 2, 1)).reshape(128, -1).astype(np.int32)
def f(rng, *shape):
    return (rng.standard_normal(shape, dtype=np.float32) * np.exp2(rng.integers(-2, 3, shape[:-1] + (1,)))).astype(BF)
def wide(rng, *shape):
    v = f(rng, *shape).astype(np.float32); k = shape[:-2] + (1, shape[-1])
    return (v * np.exp2(rng.integers(-6, 7, k)) * (rng.random(k) > 0.0625)).astype(BF)
LV, M, S = 5, 768, 48
R, A = LV * M, (LV - 1) * (N - 1) * S
W, K = R + A, 4 * M * (LV - 1)
LEV4 = np.repeat(np.concatenate([np.arange(R) // M, np.arange(A) // ((N - 1) * S)]), 4)
OWN4 = np.repeat(np.arange(W) < R, 4).astype(np.float64)
def draw_ent(rng, pri, tidy):
    e = np.zeros((8, LV - 1, 4, M), np.int64)
    for g in range(8):
        free = np.ones(4 * W, bool)
        for l in range(1, LV):
            c = np.flatnonzero(free & (LEV4 < l)); c = c[np.argsort(pri[c] + rng.random(len(c)))[:4 * M]]; free[c] = False
            e[g, l - 1] = np.sort(c).reshape(M, 4)[rng.permutation(M)].T if tidy else rng.permutation(c).reshape(4, M)
    return gtable(e.reshape(8, -1))
def draw_sl(rng, same):
    s = np.zeros((8, LV - 1, N - 1, S), np.int64)
    for g in range(8):
        for l in range(LV - 1):
            if same:
                u = np.concatenate([[0, M - 1], 1 + rng.permutation(M - 2)[:S - 2]]); v = [rng.permutation(u) for d in range(N - 1)]
            else:
                v = [rng.permutation(M)[:S] for d in range(N - 1)]
            s[g, l] = l * M + np.stack(v)
    return gtable(s.reshape(8, -1))
def draw(rng, pri, tidy, same):
    return {"b": f(rng, N, 128, R), "val": ((rng.random((N, 8, K)) - 0.5) * 0.5).astype(BF),
            "ent": np.stack([draw_ent(rng, pri[r], tidy[r]) for r in range(N)]), "sl": np.stack([draw_sl(rng, same) for r in range(N)])}
def setup_inputs(rng):
    return draw(rng, [0 * OWN4] * N, [False] * N, False)
def setup_inputs_same(rng):
    return draw(rng, [OWN4] * N, [False] * N, True)
def setup_inputs_old(rng):
    return draw(rng, [LEV4.astype(np.float64)] * N, [False] * N, False)
def setup_inputs_mixed(rng):
    o = int(rng.integers(0, 2))
    return draw(rng, [1 - OWN4 if (r + o) % 2 else OWN4 for r in range(N)], [(r + o) % 2 == 1 for r in range(N)], False)
def setup_inputs_strong(rng):
    d = setup_inputs(rng); d["val"] = np.where(rng.random((N, 8, K)) < 0.9, -0.25, 0.25).astype(BF); return d
def setup_inputs_spread(rng):
    d = setup_inputs(rng); d["b"] = wide(rng, N, 128, R)
    d["val"] = (d["val"].astype(np.float32) * np.exp2(-rng.integers(0, 7, (N, 8, K))) * (rng.random((N, 8, K)) > 0.0625)).astype(BF); return d
def check_inputs(d):
    bad = []
    if not np.isfinite(d["b"].astype(np.float32)).all(): bad.append("b finite")
    if not (np.abs(d["val"].astype(np.float32)) <= 0.25).all(): bad.append("size of val")
    lv = np.arange(LV - 1)
    for r in range(N):
        e = gentries(d["ent"][r]).astype(np.int64); s = gentries(d["sl"][r]).astype(np.int64).reshape(8, LV - 1, N - 1, S)
        if (e < 0).any() or (e >= 4 * W).any(): bad.append("ent range")
        elif (LEV4[e].reshape(8, LV - 1, 4 * M) > lv[:, None]).any(): bad.append("ent level")
        if (np.diff(np.sort(e, axis=1), axis=1) == 0).any(): bad.append("ent differ")
        if (s // M != lv[:, None, None]).any(): bad.append("sl level")
        if (np.diff(np.sort(s, axis=3), axis=3) == 0).any(): bad.append("sl differ")
    return sorted(set(bad))
def reference(b, val, ent, sl):
    en = np.stack([gentries(ent[r]) for r in range(N)]).astype(np.int64).reshape(N, 8, LV - 1, 4, M); place = en // 4
    se = np.stack([gentries(sl[r]) for r in range(N)]).astype(np.int64).reshape(N, 8, LV - 1, N - 1, S)
    v = val.astype(np.float64).reshape(N, 8, LV - 1, 4, M)
    w = np.zeros((N, 8, 16, W), np.float64); w[..., :R] = b.astype(np.float64).reshape(N, 8, 16, R)
    for l in range(LV):
        for r in range(N):
            for g in range(8):
                if l > 0: w[r, g, :, l * M:(l + 1) * M] -= np.sum(v[r, g, l - 1] * w[r, g][:, place[r, g, l - 1]], axis=1)
                if l < LV - 1:
                    for d in range(N - 1):
                        m = R + (l * (N - 1) + d) * S
                        w[(r + 1 + d) % N, g, :, m:m + S] = w[r, g][:, se[r, g, l, d]]
    z = np.zeros((N, 8, 16, R), np.float64); bk = np.zeros((N, 8, 16, 4 * W), np.float64)
    for l in range(LV - 1, -1, -1):
        for r in range(N):
            for g in range(8):
                x = w[r, g, :, l * M:(l + 1) * M] - np.sum(bk[r, g, :, 4 * l * M:4 * (l + 1) * M].reshape(16, M, 4), axis=2)
                if l < LV - 1:
                    for d in range(N - 1):
                        m = R + (l * (N - 1) + d) * S
                        x[:, se[r, g, l, d] - l * M] -= np.sum(bk[(r + 1 + d) % N, g, :, 4 * m:4 * (m + S)].reshape(16, S, 4), axis=2)
                z[r, g, :, l * M:(l + 1) * M] = x
                if l > 0: bk[r, g][:, en[r, g, l - 1]] = v[r, g, l - 1] * x[:, None, :]
    return {"z": z.reshape(N, 128, R).astype(np.float32)}

@@ -1,0 +1,381 @@
+from concourse.bass import DstId, RemoteDMATransfer
+from concourse.mybir import AluOpType, ActivationFunctionType
+
+LV, M, S, N = 5, 768, 48, 4
+R, SH = LV * M, (N - 1) * S
+K = 4 * M
+RS = 4 * R
+NV = 1024
+CH = ((1024, 1792), (1792, 2560), (2560, 3072))
+PB = 512
+TC = 208
+VC = M - TC
+VZ, GZ = 1536, 2688
+
+SCRATCH = {
+    "w": ("sbuf", [128, R + 4 * SH], "float32"),
+    "bk": ("sbuf", [128, 4 * (R + 4 * SH)], "float32"),
+    "valf": ("sbuf", [128, 4 * K], "float32"),
+    "bsb": ("sbuf", [128, R], "bfloat16"),
+    "vsb": ("sbuf", [128, 4 * K], "bfloat16"),
+    "ents": ("sbuf", [128, 768], "int32"),
+    "offf": ("sbuf", [128, 768], "uint16"),
+    "offb": ("sbuf", [128, 768], "uint16"),
+    "slr": ("sbuf", [128, 36], "int32"),
+    "slq": ("sbuf", [128, 36], "int32"),
+    "sla": ("sbuf", [128, 40], "uint16"),
+    "slb": ("sbuf", [128, 40], "uint16"),
+    "prod": ("sbuf", [128, K], "float32"),
+    "raw": ("sbuf", [128, K - NV], "float32"),
+    "zrep": ("sbuf", [128, 2 * M], "float32"),
+    "bsh": ("sbuf", [128, 4 * SH], "float32"),
+    "c0": ("sbuf", [128, SH], "float32"),
+    "c1": ("sbuf", [128, SH], "float32"),
+    "c2": ("sbuf", [128, SH], "float32"),
+    "sh": ("sbuf", [128, 4 * SH], "float32"),
+    "rsum": ("sbuf", [128, 4 * SH], "float32"),
+    "rc": ("sbuf", [128, 4 * SH], "float32"),
+    "u1": ("sbuf", [128, 2 * SH], "float32"),
+    "tmp": ("sbuf", [128, S], "float32"),
+    "negb": ("sbuf", [128, 128], "bfloat16"),
+    "sel0": ("sbuf", [128, 128], "bfloat16"),
+    "sel": ("sbuf", [128, 128], "bfloat16"),
+    "oneb": ("sbuf", [128, 128], "bfloat16"),
+    "idb": ("sbuf", [128, 128], "bfloat16"),
+    "onef": ("sbuf", [128, 128], "float32"),
+    "idf": ("sbuf", [128, 128], "float32"),
+    "acc": ("psum", [128, 2 * PB], "float32"),
+    "fac": ("psum", [128, 4 * PB], "float32"),
+    "stg": ("psum", [128, 2 * PB], "float32"),
+}
+SEMAPHORES = (["vs", "ss", "ts", "gs", "loc", "st", "ldsl"]
+              + ["ldb%d" % l for l in range(5)] + ["lde%d" % l for l in range(1, 5)]
+              + ["ldv%d" % l for l in range(1, 5)] + ["fa%d" % h for h in range(4)]
+              + ["ba%d_%d" % (h, d) for h in range(4) for d in range(3)])
+
+
+def engine_plan(src, dsts, topo):
+    left = sorted(dsts, key=lambda c: len(topo.engines(src, c)))
+    used, plan = set(), {}
+    for i, c in enumerate(left):
+        free = [e for e in topo.engines(src, c) if e not in used]
+        share = sum(1 for x in left[i:] if set(topo.engines(src, x)) == set(topo.engines(src, c)))
+        n = 1
+        while 2 * n <= len(free) // share and 2 * n <= 4:
+            n *= 2
+        plan[c] = free[:n]
+        used.update(plan[c])
+    return plan
+
+
+def rank_program(g, core, T, topo):
+    rank = T.rank_of(core)
+    if rank is None:
+        return
+    ADD, MUL = AluOpType.add, AluOpType.mult
+    COPY = ActivationFunctionType.Copy
+    cores = list(T.cores)
+    q = {"v": g.vector, "s": g.scalar, "t": g.tensor, "g": g, "y": g.sync}
+    own = {"v": "vs", "s": "ss", "t": "ts", "g": "gs"}
+    count = {"vs": 0, "ss": 0, "ts": 0, "gs": 0}
+    seen = {k: {} for k in q}
+
+    def wait(k, *tokens):
+        need = {}
+        for name, n in tokens:
+            if n > need.get(name, 0):
+                need[name] = n
+        for name, n in need.items():
+            if n > seen[k].get(name, 0):
+                q[k].wait_ge(T.sem[name], n)
+                seen[k][name] = n
+
+    def done(k, ins):
+        name = own[k]
+        ins.then_inc(T.sem[name], 1)
+        count[name] += 1
+        return (name, count[name])
+
+    def copy(out, in_):
+        return done("s", g.scalar.activation(out, in_, COPY))
+
+    others = [c for c in cores if c != core]
+    plan = engine_plan(core, others, topo)
+    arrive = {c: len(engine_plan(c, [x for x in cores if x != c], topo)[core]) for c in others}
+
+    def send(h, src, dst, dst_base, forward):
+        tr = []
+        for d in range(3):
+            c = cores[(rank + 1 + d) % N] if forward else cores[(rank - 1 - d) % N]
+            rid, pid = topo.addr(c)[:2]
+            a = (h * 3 + d) * S
+            m = sum(1 << e for e in plan[c])
+            sem = T.sem["fa%d" % h] if forward else T.sem["ba%d_%d" % (h, d)]
+            tr.append(RemoteDMATransfer(dst_ids=[DstId(rid=rid, pnc=pid)], dma_engine_mask=m, remote_sem=sem,
+                                        srcs=[src[:, a:a + S]], dsts=[dst[:, dst_base + a:dst_base + a + S]]))
+        g.remote_dma_fused(tr, local_sem=T.sem["loc"])
+
+    local_each = sum(len(e) for e in plan.values())
+    fa = {h: ("fa%d" % h, sum(arrive.values())) for h in range(4)}
+    ba = {(h, d): ("ba%d_%d" % (h, d), arrive[cores[(rank + 1 + d) % N]]) for h in range(4) for d in range(3)}
+
+    def load(k, name, out, in_):
+        q[k].dma_start(out, in_).then_inc(T.sem[name], 16)
+
+    def ld_b(k, l):
+        load(k, "ldb%d" % l, T.bsb[:, l * M:(l + 1) * M], T.b[:, l * M:(l + 1) * M])
+
+    def ld_e(k, l):
+        a = 192 * (l - 1)
+        load(k, "lde%d" % l, T.ents[:, a:a + 192], T.ent[:, a:a + 192])
+
+    def ld_v(k, l):
+        a = K * (l - 1)
+        load(k, "ldv%d" % l, T.vsb[0:8, a:a + K], T.val[:, a:a + K])
+
+    load("s", "ldsl", T.slr[:, :], T.sl[:, :])
+    ld_b("y", 0)
+    wait("y", ("ldsl", 16))
+    ld_v("y", 1)
+    ld_e("y", 1)
+    ld_b("y", 1)
+
+    v = g.vector
+    k_neg = done("v", v.memset(T.negb[:, :], -1.0))
+    k_oneb = done("v", v.memset(T.oneb[:, :], 1.0))
+    k_onef = done("v", v.memset(T.onef[:, :], 1.0))
+    k_wz = done("v", v.memset(T.w[:, 2304:3840], 0.0))
+    wait("g", k_neg)
+    x = done("g", g.affine_select(T.sel0[0:8, :], T.negb[0:8, :], [[1, 128]], AluOpType.is_ge, 0.0, 0, -16))
+    wait("g", x)
+    k_sel = done("g", g.affine_select(T.sel[0:8, :], T.sel0[0:8, :], [[-1, 128]], AluOpType.is_ge, 0.0, 15, 16))
+    wait("g", k_oneb)
+    k_idb = done("g", g.affine_select(T.idb[:, :], T.oneb[:, :], [[-1, 128]], AluOpType.is_equal, 0.0, 0, 1))
+    wait("g", k_onef)
+    k_idf = done("g", g.affine_select(T.idf[:, :], T.onef[:, :], [[-1, 128]], AluOpType.is_equal, 0.0, 0, 1))
+    wait("s", k_wz)
+    k_wz2 = copy(T.w[:, 768:2304], T.w[:, 2304:3840])
+
+    wait("v", ("ldsl", 16))
+    k_sl = done("v", v.tensor_copy(T.sla[:, 0:9], T.slr[:, 0:9]))
+
+    def sl_cols(h, d, n):
+        c = h * 9 + d * 3
+        return T.sla[:, c:c + n] if c % 2 == 0 else T.slb[:, c + 1:c + 1 + n]
+
+    wait("v", ("ldb0", 16), k_sl)
+    k_sh = done("v", v.tensor_copy(T.sh[:, 0:SH], T.bsb[:, 0:M].indirect(sl_cols(0, 0, 9))))
+    wait("g", k_sh)
+    send(0, T.sh, T.w, R, True)
+
+    k_bz = []
+
+    def g_zero(h):
+        a = VZ + GZ * h
+        k_bz.append(done("g", g.iota(T.bk[:, a:a + GZ], [[0, GZ]], 0, 0, allow_small_or_imprecise_dtypes=True)))
+
+    g_zero(0)
+
+    wait("s", ("ldb0", 16))
+    k_y = {0: copy(T.w[:, 0:M], T.bsb[:, 0:M])}
+
+    k_off, k_offb = {}, {}
+
+    def lists(l):
+        a = 192 * (l - 1)
+        wait("v", ("lde%d" % l, 16))
+        k_off[l] = done("v", v.tensor_scalar(T.offf[:, a:a + 192], T.ents[:, a:a + 192], 0.25, -0.375, MUL, ADD))
+
+    def slots(l):
+        a = 192 * (l - 1)
+        k_offb[l] = done("v", v.tensor_copy(T.offb[:, a:a + 192], T.ents[:, a:a + 192]))
+
+    for h in range(1, 4):
+        x = done("v", v.tensor_scalar(T.slq[:, 9 * h:9 * h + 9], T.slr[:, 9 * h:9 * h + 9], -M * h, None, ADD))
+    done("v", v.tensor_copy(T.slb[:, 1:10], T.slr[:, 0:9]))
+    wait("v", x)
+    done("v", v.tensor_copy(T.sla[:, 9:36], T.slq[:, 9:36]))
+    k_sl = done("v", v.tensor_copy(T.slb[:, 10:37], T.slq[:, 9:36]))
+    k_bz0 = done("v", v.memset(T.bk[:, 0:VZ], 0.0))
+    k_bz.append(k_bz0)
+    lists(1)
+
+    k_fac, k_cst, k_cfac, k_m, k_a3 = {}, {}, {}, {}, {}
+    banks = ((0, PB), (PB, M))
+    stage = ((0, PB), (PB, NV))
+    quarters = tuple((a, a + PB) for a in range(0, K - NV, PB))
+
+    def prep_stage(l):
+        base = K * (l - 1)
+        wait("t", k_sel, ("ldv%d" % l, 16))
+        if l > 1:
+            wait("t", k_cst[l - 1])
+        for a, e in stage:
+            k = done("t", g.tensor.matmul(T.stg[:, a:e], T.sel[0:8, :], T.vsb[0:8, base + a:base + e], True, True))
+            wait("s", k)
+            k_cst[l] = copy(T.valf[:, base + a:base + e], T.stg[:, a:e])
+
+    def prep_fac(l):
+        for a, e in quarters:
+            k_fac[l] = done("t", g.tensor.matmul(T.fac[:, a:e], T.sel[0:8, :], T.vsb[0:8, K * (l - 1) + NV + a:K * (l - 1) + NV + e], True, True))
+
+    def copy_fac(l):
+        for a, e in quarters:
+            k_cfac[l] = copy(T.valf[:, K * (l - 1) + NV + a:K * (l - 1) + NV + e], T.fac[:, a:e])
+
+    def prep_acc(l):
+        wait("t", k_idb, ("ldb%d" % l, 16))
+        if l > 1:
+            wait("t", k_a3[l - 1])
+        for a, e in banks:
+            done("t", g.tensor.matmul(T.acc[:, a:e], T.idb[:, :], T.bsb[:, l * M + a:l * M + e], True, False))
+
+    def shown_b(l):
+        wait("s", ("ldb%d" % l, 16), k_sl)
+        return copy(T.bsh[:, l * SH:(l + 1) * SH], T.bsb[:, l * M:(l + 1) * M].indirect(sl_cols(l, 0, 9)))
+
+    prep_stage(1)
+    prep_fac(1)
+    prep_acc(1)
+    k_bsh = shown_b(1)
+
+    for l in range(1, 5):
+        win = T.w[:, 0:R + SH * l]
+        blk = [T.prod[:, e * M:(e + 1) * M] for e in range(4)]
+        base, col = K * (l - 1), 192 * (l - 1)
+        k_raw = []
+        wait("s", fa[l - 1], k_off[l], k_wz, k_wz2, k_y[l - 1])
+        for a, e in CH:
+            k_raw.append(copy(T.raw[:, a - NV:e - NV], win.indirect(T.offf[:, col + a // 16:col + e // 16])))
+        wait("v", fa[l - 1], k_off[l], k_wz, k_wz2, k_cst[l], k_y[l - 1])
+        if l < 4:
+            k_p = [done("v", v.tensor_tensor(T.prod[:, 0:NV], win.indirect(T.offf[:, col:col + NV // 16]), T.valf[:, base:base + NV], MUL))]
+        else:
+            k_p = [done("v", v.tensor_tensor(blk[0], win.indirect(T.offf[:, col:col + M // 16]), T.valf[:, base:base + M], MUL))]
+            done("v", v.tensor_tensor(T.prod[:, M:NV], win.indirect(T.offf[:, col + M // 16:col + NV // 16]), T.valf[:, base + M:base + NV], MUL))
+
+        def product(i):
+            a, e = CH[i]
+            wait("v", k_raw[i], k_fac[l])
+            k_p.append(done("v", v.tensor_tensor(T.prod[:, a:e], T.raw[:, a - NV:e - NV], T.fac[:, a - NV:e - NV], MUL)))
+
+        cs = [T.bsh[:, l * SH:(l + 1) * SH], T.c0[:, :], T.c1[:, :], T.c2[:, :], T.sh[:, l * SH:(l + 1) * SH]] if l < 4 else None
+        k_c = [k_bsh]
+
+        def shown(e):
+            wait("v", k_sl, k_p[e], k_c[-1])
+            k_c.append(done("v", v.tensor_tensor(cs[e + 1], blk[e].indirect(sl_cols(l, 0, 9)), cs[e], ADD)))
+
+        product(0)
+        if l < 4:
+            shown(0)
+        product(1)
+        if l < 4:
+            shown(1)
+        product(2)
+        k_m[l] = k_p[3]
+        if l < 4:
+            shown(2)
+            shown(3)
+            wait("g", k_c[-1])
+            send(l, T.sh, T.w, R, True)
+            g_zero(l)
+
+        def tensor_add(a, e, i, last):
+            wait("t", k_p[i], k_idf)
+            return done("t", g.tensor.matmul(T.acc[:, a:e], T.idf[:, :], T.prod[:, i * M + a:i * M + e], False, last))
+
+        k_acc0 = tensor_add(0, PB, 0, True)
+        tensor_add(PB, M, 0, False)
+        k_acc1 = tensor_add(PB, M, 1, True)
+        if l < 4:
+            wait("y", fa[l - 1])
+            ld_v("y", l + 1)
+            ld_b("y", l + 1)
+            ld_e("y", l + 1)
+            wait("s", k_bz0)
+            a = RS + M * (l - 1)
+            k_bz.append(copy(T.bk[:, a:a + M], T.bk[:, 0:M]))
+            prep_stage(l + 1)
+            if l < 3:
+                k_bsh = shown_b(l + 1)
+
+        def vector_add(a, e, i, *need):
+            wait("v", k_p[i], *need)
+            out = T.acc[:, a:e] if i < 3 else T.w[:, l * M + a:l * M + e]
+            return done("v", v.tensor_tensor(out, T.acc[:, a:e], T.prod[:, i * M + a:i * M + e], ADD))
+
+        k_h = [k_acc0, k_acc0]
+        for i in range(1, 4):
+            for h in range(2):
+                k_h[h] = vector_add(h * PB // 2, (h + 1) * PB // 2, i, k_h[h])
+        k_acc1 = vector_add(PB, M, 2, k_acc1)
+        k_a3[l] = k_y[l] = vector_add(PB, M, 3, k_acc1)
+        if l < 4:
+            wait("t", k_m[l])
+            prep_fac(l + 1)
+            prep_acc(l + 1)
+            lists(l + 1)
+        else:
+            wait("s", k_m[4])
+            copy_fac(4)
+    slots(4)
+
+    k_z = k_a3[4]
+    stores = 0
+    for l in range(4, -1, -1):
+        if l < 4:
+            a = RS + 4 * SH * l
+            x = done("v", v.tensor_tensor(T.u1[:, :], T.bk[:, a:a + 4 * SH:2], T.bk[:, a + 1:a + 4 * SH:2], ADD))
+            wait("v", x)
+            k_rs = done("v", v.tensor_tensor(T.rsum[:, l * SH:(l + 1) * SH], T.u1[:, 0:2 * SH:2], T.u1[:, 1:2 * SH:2], ADD))
+            wait("g", k_rs)
+            send(l, T.rsum, T.rc, 0, False)
+            wait("t", k_sc, k_cst[4])
+            for s in range(4):
+                k_t = done("t", g.tensor.matmul(T.stg[:, 0:TC], T.idf[:, :], T.bk[:, K * l + 4 * VC + s:K * (l + 1):4], s == 0, s == 3))
+            k_h = [k_yc, k_yc]
+            for s in range(4):
+                for h, (a, e) in enumerate(((0, VC // 2), (VC // 2, VC))):
+                    wait("v", k_h[h])
+                    out = T.acc[:, a:e] if s < 3 else T.w[:, l * M + a:l * M + e]
+                    k_h[h] = done("v", v.tensor_tensor(out, T.acc[:, a:e], T.bk[:, K * l + 4 * a + s:K * l + 4 * e:4], ADD))
+            if l > 0:
+                slots(l)
+            wait("v", k_t)
+            tail = T.w[:, l * M + VC:(l + 1) * M]
+            x = done("v", v.tensor_tensor(tail, T.stg[:, 0:TC], tail, ADD))
+            wait("v", x)
+            ds = sorted(range(3), key=lambda d: topo.chip(cores[(rank + 1 + d) % N]) != topo.chip(core))
+            win = T.w[:, M * l:M * (l + 1)]
+            for d in ds:
+                a = (l * 3 + d) * S
+                wait("v", ba[l, d])
+                x = done("v", v.tensor_tensor(T.tmp[:, :], win.indirect(sl_cols(l, d, 3)), T.rc[:, a:a + S], ADD))
+                wait("v", x)
+                k_z = done("v", v.tensor_copy(win.indirect(sl_cols(l, d, 3)), T.tmp[:, :]))
+                wait("v", k_z)
+        zl = T.w[:, l * M:(l + 1) * M]
+        wait("y", k_z)
+        g.sync.dma_start(T.z[:, l * M:(l + 1) * M], zl).then_inc(T.sem["st"], 16)
+        stores += 16
+        if l > 0:
+            wait("s", k_z)
+            copy(T.zrep[:, 0:M], zl)
+            k_rep = copy(T.zrep[:, M:2 * M], zl)
+            k_yc = copy(T.acc[:, 0:VC], T.w[:, (l - 1) * M:(l - 1) * M + VC])
+            base, col = K * (l - 1), 192 * (l - 1)
+            bwin = T.bk[:, 0:RS + 4 * SH * l]
+            for a, e, src, need in ((0, M, zl, [k_z, k_offb[l], k_cst[4]] + k_bz), (M, 2 * M, zl, [k_cfac[l]]),
+                                    (2 * M, K, T.zrep[:, :], [k_rep])):
+                wait("v", *need)
+                k_sc = done("v", v.tensor_tensor(bwin.indirect(T.offb[:, col + a // 16:col + e // 16]), src, T.valf[:, base + a:base + e], MUL))
+                wait("v", k_sc)
+            if l > 1:
+                wait("t", k_cfac[l])
+                prep_fac(l - 1)
+                wait("s", k_fac[l - 1])
+                copy_fac(l - 1)
+    g.sync.wait_ge(T.sem["st"], stores)
+    g.wait_ge(T.sem["loc"], 8 * local_each)
+    wait("v", ("ss", count["ss"]), ("ts", count["ts"]), ("gs", count["gs"]))

@@ -4,30 +4,47 @@ from concourse.mybir import AluOpType, ActivationFunctionType
 LV, M, S, N = 5, 768, 48, 4
 R, SH = LV * M, (N - 1) * S
 K = 4 * M
-RS = 4 * R
-NV = 1024
-CH = ((1024, 1792), (1792, 2560), (2560, 3072))
+QN = (R + 4 * SH) // 16
 PB = 512
-TC = 208
-VC = M - TC
-VZ, GZ = 1536, 2688
+PAD, LIFT = 8, 32
+NV = M
+CH = ((768, 1536), (1536, 2304), (2304, 2816), (2816, 3072))
+VA = 384
+COPIER = "svvv"
+POS = (768, 192, 96, 0, 0)
+AFTER = False
+TA = ((1, 2), (1, 2), (1, 2), (1, 2))
+TB = 2
+FOLD = 4
+WIDE = 8
+SLOTS = (0, 1792, 1920, 2048, 2432, 2048, 2048)
+SNAPS = {2: 3, 4: 2, 5: 1, 6: 0}
+IOTAS = (0, 1792, 1920, 2048, 4480, 2048)
+PIECE = 1024
 
 SCRATCH = {
     "w": ("sbuf", [128, R + 4 * SH], "float32"),
-    "bk": ("sbuf", [128, 4 * (R + 4 * SH)], "float32"),
-    "valf": ("sbuf", [128, 4 * K], "float32"),
+    "inv": ("sbuf", [128, 6 * K], "float32"),
+    "invo": ("sbuf", [128, 768], "float32"),
+    "invr": ("sbuf", [128, 4, 4, 48], "float32"),
+    "pr": ("sbuf", [128, PAD + 4 * K], "float32"),
+    "valf": ("sbuf", [128, K], "bfloat16"),
+    "nid": ("sbuf", [128, 128], "float32"),
     "bsb": ("sbuf", [128, R], "bfloat16"),
     "vsb": ("sbuf", [128, 4 * K], "bfloat16"),
     "ents": ("sbuf", [128, 768], "int32"),
+    "e1": ("sbuf", [128, 768], "int32"),
+    "e2": ("sbuf", [128, 768], "int32"),
     "offf": ("sbuf", [128, 768], "uint16"),
-    "offb": ("sbuf", [128, 768], "uint16"),
+    "pos": ("sbuf", [128, 768], "uint16"),
+    "offo": ("sbuf", [128, 768], "uint16"),
+    "offr": ("sbuf", [128, 144], "uint16"),
     "slr": ("sbuf", [128, 36], "int32"),
     "slq": ("sbuf", [128, 36], "int32"),
     "sla": ("sbuf", [128, 40], "uint16"),
     "slb": ("sbuf", [128, 40], "uint16"),
     "prod": ("sbuf", [128, K], "float32"),
-    "raw": ("sbuf", [128, K - NV], "float32"),
-    "zrep": ("sbuf", [128, 2 * M], "float32"),
+    "raw": ("sbuf", [128, max(K - NV, 4 * (M - VA))], "float32"),
     "bsh": ("sbuf", [128, 4 * SH], "float32"),
     "c0": ("sbuf", [128, SH], "float32"),
     "c1": ("sbuf", [128, SH], "float32"),
@@ -36,6 +53,7 @@ SCRATCH = {
     "rsum": ("sbuf", [128, 4 * SH], "float32"),
     "rc": ("sbuf", [128, 4 * SH], "float32"),
     "u1": ("sbuf", [128, 2 * SH], "float32"),
+    "u2": ("sbuf", [128, 2 * SH], "float32"),
     "tmp": ("sbuf", [128, S], "float32"),
     "negb": ("sbuf", [128, 128], "bfloat16"),
     "sel0": ("sbuf", [128, 128], "bfloat16"),
@@ -45,35 +63,44 @@ SCRATCH = {
     "onef": ("sbuf", [128, 128], "float32"),
     "idf": ("sbuf", [128, 128], "float32"),
     "acc": ("psum", [128, 2 * PB], "float32"),
-    "fac": ("psum", [128, 4 * PB], "float32"),
-    "stg": ("psum", [128, 2 * PB], "float32"),
+    "fac": ("psum", [128, 6 * PB], "float32"),
 }
-SEMAPHORES = (["vs", "ss", "ts", "gs", "loc", "st", "ldsl"]
-              + ["ldb%d" % l for l in range(5)] + ["lde%d" % l for l in range(1, 5)]
-              + ["ldv%d" % l for l in range(1, 5)] + ["fa%d" % h for h in range(4)]
+SEMAPHORES = (["vs", "ss", "ts", "gs", "st", "ldsl", "ini"] + ["loc%d" % i for i in range(8)]
+              + ["snap%d" % i for i in SNAPS]
+              + ["ldb%d" % l for l in range(5)] + ["lde"]
+              + ["ldv%d" % l for l in range(1, 5)] + ["ldf%d" % l for l in range(3, 5)] + ["fa%d" % h for h in range(4)]
               + ["ba%d_%d" % (h, d) for h in range(4) for d in range(3)])
 
 
-def engine_plan(src, dsts, topo):
+def engine_plan(src, dsts, topo, most):
     left = sorted(dsts, key=lambda c: len(topo.engines(src, c)))
     used, plan = set(), {}
     for i, c in enumerate(left):
         free = [e for e in topo.engines(src, c) if e not in used]
         share = sum(1 for x in left[i:] if set(topo.engines(src, x)) == set(topo.engines(src, c)))
         n = 1
-        while 2 * n <= len(free) // share and 2 * n <= 4:
+        while 2 * n <= len(free) // share and 2 * n <= most:
             n *= 2
         plan[c] = free[:n]
         used.update(plan[c])
     return plan
 
 
+def pieces(a, e):
+    out = []
+    while a < e:
+        x = min(e, a + PIECE, (a // K + 1) * K)
+        out.append((a, x))
+        a = x
+    return out
+
+
 def rank_program(g, core, T, topo):
     rank = T.rank_of(core)
     if rank is None:
         return
-    ADD, MUL = AluOpType.add, AluOpType.mult
-    COPY = ActivationFunctionType.Copy
+    ADD, SUB, MUL = AluOpType.add, AluOpType.subtract, AluOpType.mult
+    COPY, SILU = ActivationFunctionType.Copy, ActivationFunctionType.Silu
     cores = list(T.cores)
     q = {"v": g.vector, "s": g.scalar, "t": g.tensor, "g": g, "y": g.sync}
     own = {"v": "vs", "s": "ss", "t": "ts", "g": "gs"}
@@ -100,24 +127,87 @@ def rank_program(g, core, T, topo):
         return done("s", g.scalar.activation(out, in_, COPY))
 
     others = [c for c in cores if c != core]
-    plan = engine_plan(core, others, topo)
-    arrive = {c: len(engine_plan(c, [x for x in cores if x != c], topo)[core]) for c in others}
+    most = {True: 4, False: WIDE}
+    plans = {f: engine_plan(core, others, topo, most[f]) for f in most}
+    arrive = {f: {c: len(engine_plan(c, [x for x in cores if x != c], topo, most[f])[core]) for c in others} for f in most}
+    left = []
 
     def send(h, src, dst, dst_base, forward):
         tr = []
+        plan = plans[forward]
+        local_each = sum(len(e) for e in plan.values())
         for d in range(3):
             c = cores[(rank + 1 + d) % N] if forward else cores[(rank - 1 - d) % N]
             rid, pid = topo.addr(c)[:2]
             a = (h * 3 + d) * S
             m = sum(1 << e for e in plan[c])
             sem = T.sem["fa%d" % h] if forward else T.sem["ba%d_%d" % (h, d)]
+            srcs = [src[:, a:a + S]] if forward else [src[:, s * SH + d * S:s * SH + (d + 1) * S] for s in range(FOLD)]
             tr.append(RemoteDMATransfer(dst_ids=[DstId(rid=rid, pnc=pid)], dma_engine_mask=m, remote_sem=sem,
-                                        srcs=[src[:, a:a + S]], dsts=[dst[:, dst_base + a:dst_base + a + S]]))
-        g.remote_dma_fused(tr, local_sem=T.sem["loc"])
+                                        srcs=srcs, dsts=[dst[:, dst_base + a:dst_base + a + S]],
+                                        alu_op=0 if forward else 1))
+        name = "loc%d" % len(left)
+        g.remote_dma_fused(tr, local_sem=T.sem[name])
+        left.append((name, local_each))
+        lay(len(left))
 
-    local_each = sum(len(e) for e in plan.values())
-    fa = {h: ("fa%d" % h, sum(arrive.values())) for h in range(4)}
-    ba = {(h, d): ("ba%d_%d" % (h, d), arrive[cores[(rank + 1 + d) % N]]) for h in range(4) for d in range(3)}
+    fa = {h: ("fa%d" % h, sum(arrive[True].values())) for h in range(4)}
+    ba = {(h, d): ("ba%d_%d" % (h, d), arrive[False][cores[(rank + 1 + d) % N]]) for h in range(4) for d in range(3)}
+
+    laid, k_pos, k_snap, k_list, k_scat = [], {}, {}, {}, {}
+    last = {"scat": [], "conv": []}
+
+    def lay(i):
+        if i < len(IOTAS):
+            a = sum(IOTAS[:i])
+            for x, e in pieces(a, a + IOTAS[i]):
+                laid.append((e, done("g", g.iota(T.pr[:, PAD + x:PAD + e], [[1, e - x]], PAD + x + LIFT, 0,
+                                                 allow_small_or_imprecise_dtypes=True))))
+
+    def positions(a, b, psum):
+        if a < b:
+            levels = range(a // 192 + 1, (b - 1) // 192 + 2)
+            e, e1, e2 = T.ents[:, a:b], T.e1[:, a:b], T.e2[:, a:b]
+            y = psum[:, 0:b - a]
+            wait("v", *[k_ent[l] for l in levels])
+            x1 = done("v", v.tensor_scalar(e1, e, 63, None, AluOpType.bitwise_and))
+            x2 = done("v", v.tensor_scalar(e2, e, 1.0 / K, 0.5 / K - 0.5, MUL, ADD))
+            wait("v", x1)
+            x1 = done("v", v.tensor_scalar(y, e1, K - 1, None, MUL))
+            wait("v", x2)
+            x2 = done("v", v.tensor_scalar(e2, e2, 63 * K, None, MUL))
+            wait("v", x1)
+            x1 = done("v", v.tensor_tensor(y, y, e, ADD))
+            wait("v", x1, x2)
+            x1 = done("v", v.tensor_tensor(e1, y, e2, ADD))
+            wait("v", x1)
+            x1 = done("v", v.tensor_scalar(T.pos[:, a:b], e1, 1.0 / 64, None, MUL))
+            k_pos.update({l: x1 for l in levels})
+
+    def scatter(i):
+        a = sum(SLOTS[:i])
+        for x, e in pieces(a, a + SLOTS[i]):
+            l = 4 - x // K
+            col = 192 * (l - 1) + (x % K) // 16
+            wait("s", ("ini", 32), k_pos[l], min(t for t in laid if t[0] >= e)[1], *last["scat"])
+            k_scat[l] = done("s", g.scalar.activation(T.inv[:, :].indirect(T.pos[:, col:col + (e - x) // 16]),
+                                                      T.pr[:, PAD + x:PAD + e], SILU))
+            last["scat"] = [k_scat[l]]
+
+    def snapshot(i, *need):
+        if i in SNAPS:
+            h = SNAPS[i]
+            wait("y", *(last["scat"] + list(need)))
+            g.sync.dma_start(T.invr[:, h, :, :], T.inv[0:128:16, 5 * K:6 * K]).then_inc(T.sem["snap%d" % i], 16)
+            g.sync.dma_start(T.invo[:, 192 * h:192 * h + 192], T.inv[0:128:16, h * K:(h + 1) * K]).then_inc(T.sem["snap%d" % i], 16)
+            k_snap[h] = ("snap%d" % i, 32)
+            last["scat"] = [k_snap[h]]
+
+    def convert(h):
+        wait("v", k_snap[h])
+        x = done("v", v.tensor_scalar(T.offr[:, 36 * h:36 * h + 36], T.invr[:, h, :, 9 * h:9 * h + 9], -LIFT, None, ADD))
+        y = done("v", v.tensor_scalar(T.offo[:, 192 * h:192 * h + 192], T.invo[:, 192 * h:192 * h + 192], -LIFT, None, ADD))
+        k_list[h] = (x, y)
 
     def load(k, name, out, in_):
         q[k].dma_start(out, in_).then_inc(T.sem[name], 16)
@@ -125,36 +215,45 @@ def rank_program(g, core, T, topo):
     def ld_b(k, l):
         load(k, "ldb%d" % l, T.bsb[:, l * M:(l + 1) * M], T.b[:, l * M:(l + 1) * M])
 
-    def ld_e(k, l):
-        a = 192 * (l - 1)
-        load(k, "lde%d" % l, T.ents[:, a:a + 192], T.ent[:, a:a + 192])
-
     def ld_v(k, l):
         a = K * (l - 1)
         load(k, "ldv%d" % l, T.vsb[0:8, a:a + K], T.val[:, a:a + K])
 
+    def ld_f(k, l):
+        for c in range(16):
+            load(k, "ldf%d" % l, T.valf[c:128:16, M * (l - 1):M * l], T.val[:, K * (l - 1):K * (l - 1) + M])
+
     load("s", "ldsl", T.slr[:, :], T.sl[:, :])
     ld_b("y", 0)
     wait("y", ("ldsl", 16))
+    load("y", "lde", T.ents[:, :], T.ent[:, :])
+    k_ent = {l: ("lde", 16) for l in range(1, 5)}
     ld_v("y", 1)
-    ld_e("y", 1)
+    ld_v("y", 2)
     ld_b("y", 1)
+
+    def clear():
+        wait("y", k_wz)
+        load("y", "ini", T.inv[0:128:16, 0:4 * K], T.w[:, 2304:2304 + M])
+        load("y", "ini", T.inv[0:128:16, 5 * K:6 * K], T.w[:, 2304:2304 + 192])
 
     v = g.vector
     k_neg = done("v", v.memset(T.negb[:, :], -1.0))
+    k_wz = done("v", v.memset(T.w[:, 2304:3840], 0.0))
     k_oneb = done("v", v.memset(T.oneb[:, :], 1.0))
     k_onef = done("v", v.memset(T.onef[:, :], 1.0))
-    k_wz = done("v", v.memset(T.w[:, 2304:3840], 0.0))
+    k_pad = done("v", v.memset(T.pr[:, 0:PAD], 0.0))
+    lay(0)
     wait("g", k_neg)
     x = done("g", g.affine_select(T.sel0[0:8, :], T.negb[0:8, :], [[1, 128]], AluOpType.is_ge, 0.0, 0, -16))
     wait("g", x)
     k_sel = done("g", g.affine_select(T.sel[0:8, :], T.sel0[0:8, :], [[-1, 128]], AluOpType.is_ge, 0.0, 15, 16))
     wait("g", k_oneb)
     k_idb = done("g", g.affine_select(T.idb[:, :], T.oneb[:, :], [[-1, 128]], AluOpType.is_equal, 0.0, 0, 1))
-    wait("g", k_onef)
-    k_idf = done("g", g.affine_select(T.idf[:, :], T.onef[:, :], [[-1, 128]], AluOpType.is_equal, 0.0, 0, 1))
     wait("s", k_wz)
     k_wz2 = copy(T.w[:, 768:2304], T.w[:, 2304:3840])
+    if SLOTS[0]:
+        clear()
 
     wait("v", ("ldsl", 16))
     k_sl = done("v", v.tensor_copy(T.sla[:, 0:9], T.slr[:, 0:9]))
@@ -165,30 +264,23 @@ def rank_program(g, core, T, topo):
 
     wait("v", ("ldb0", 16), k_sl)
     k_sh = done("v", v.tensor_copy(T.sh[:, 0:SH], T.bsb[:, 0:M].indirect(sl_cols(0, 0, 9))))
+    wait("g", k_onef)
+    k_idf = done("g", g.affine_select(T.idf[:, :], T.onef[:, :], [[-1, 128]], AluOpType.is_equal, 0.0, 0, 1))
     wait("g", k_sh)
     send(0, T.sh, T.w, R, True)
-
-    k_bz = []
-
-    def g_zero(h):
-        a = VZ + GZ * h
-        k_bz.append(done("g", g.iota(T.bk[:, a:a + GZ], [[0, GZ]], 0, 0, allow_small_or_imprecise_dtypes=True)))
-
-    g_zero(0)
+    if not SLOTS[0]:
+        wait("y", left[0])
+        clear()
 
     wait("s", ("ldb0", 16))
     k_y = {0: copy(T.w[:, 0:M], T.bsb[:, 0:M])}
 
-    k_off, k_offb = {}, {}
+    k_off = {}
 
     def lists(l):
         a = 192 * (l - 1)
-        wait("v", ("lde%d" % l, 16))
+        wait("v", ("lde", 16))
         k_off[l] = done("v", v.tensor_scalar(T.offf[:, a:a + 192], T.ents[:, a:a + 192], 0.25, -0.375, MUL, ADD))
-
-    def slots(l):
-        a = 192 * (l - 1)
-        k_offb[l] = done("v", v.tensor_copy(T.offb[:, a:a + 192], T.ents[:, a:a + 192]))
 
     for h in range(1, 4):
         x = done("v", v.tensor_scalar(T.slq[:, 9 * h:9 * h + 9], T.slr[:, 9 * h:9 * h + 9], -M * h, None, ADD))
@@ -196,37 +288,24 @@ def rank_program(g, core, T, topo):
     wait("v", x)
     done("v", v.tensor_copy(T.sla[:, 9:36], T.slq[:, 9:36]))
     k_sl = done("v", v.tensor_copy(T.slb[:, 10:37], T.slq[:, 9:36]))
-    k_bz0 = done("v", v.memset(T.bk[:, 0:VZ], 0.0))
-    k_bz.append(k_bz0)
+    wait("v", k_idf)
+    k_nid = done("v", v.tensor_scalar(T.nid[:, :], T.idf[:, :], -1.0, None, MUL))
     lists(1)
+    positions(POS[1], POS[0], T.acc)
 
-    k_fac, k_cst, k_cfac, k_m, k_a3 = {}, {}, {}, {}, {}
+    k_fac, k_stg, k_cst, k_m, k_a3 = {}, {}, {}, {}, {}
     banks = ((0, PB), (PB, M))
-    stage = ((0, PB), (PB, NV))
-    quarters = tuple((a, a + PB) for a in range(0, K - NV, PB))
 
-    def prep_stage(l):
-        base = K * (l - 1)
+    def factors(l, a, e):
         wait("t", k_sel, ("ldv%d" % l, 16))
-        if l > 1:
-            wait("t", k_cst[l - 1])
-        for a, e in stage:
-            k = done("t", g.tensor.matmul(T.stg[:, a:e], T.sel[0:8, :], T.vsb[0:8, base + a:base + e], True, True))
-            wait("s", k)
-            k_cst[l] = copy(T.valf[:, base + a:base + e], T.stg[:, a:e])
-
-    def prep_fac(l):
-        for a, e in quarters:
-            k_fac[l] = done("t", g.tensor.matmul(T.fac[:, a:e], T.sel[0:8, :], T.vsb[0:8, K * (l - 1) + NV + a:K * (l - 1) + NV + e], True, True))
-
-    def copy_fac(l):
-        for a, e in quarters:
-            k_cfac[l] = copy(T.valf[:, K * (l - 1) + NV + a:K * (l - 1) + NV + e], T.fac[:, a:e])
+        while a < e:
+            x = (a // PB + 1) * PB
+            k = done("t", g.tensor.matmul(T.fac[:, a:x], T.sel[0:8, :], T.vsb[0:8, K * (l - 1) + a:K * (l - 1) + x], True, True))
+            a = x
+        return k
 
     def prep_acc(l):
-        wait("t", k_idb, ("ldb%d" % l, 16))
-        if l > 1:
-            wait("t", k_a3[l - 1])
+        wait("t", k_idb, ("ldb%d" % l, 16), *([k_a3[l - 1]] if l > 1 else k_pos.values()))
         for a, e in banks:
             done("t", g.tensor.matmul(T.acc[:, a:e], T.idb[:, :], T.bsb[:, l * M + a:l * M + e], True, False))
 
@@ -234,148 +313,177 @@ def rank_program(g, core, T, topo):
         wait("s", ("ldb%d" % l, 16), k_sl)
         return copy(T.bsh[:, l * SH:(l + 1) * SH], T.bsb[:, l * M:(l + 1) * M].indirect(sl_cols(l, 0, 9)))
 
-    prep_stage(1)
-    prep_fac(1)
+    k_f = {l: ("ldf%d" % l, 256) for l in range(3, 5)}
+    for l, a in ((1, 0), (2, 2 * PB)):
+        wait("t", k_sel, ("ldv%d" % l, 16))
+        for x, e in banks:
+            k = done("t", g.tensor.matmul(T.fac[:, a + x:a + e], T.sel[0:8, :], T.vsb[0:8, K * (l - 1) + x:K * (l - 1) + e], True, True))
+        wait("s", k)
+        k_f[l] = done("s", g.scalar.activation(T.valf[:, M * (l - 1):M * l], T.fac[:, a:a + M], COPY, scale=-1.0))
+    wait("t", k_f[2])
+    k_fac[1] = factors(1, NV, K)
     prep_acc(1)
     k_bsh = shown_b(1)
+    scatter(0)
 
     for l in range(1, 5):
         win = T.w[:, 0:R + SH * l]
         blk = [T.prod[:, e * M:(e + 1) * M] for e in range(4)]
-        base, col = K * (l - 1), 192 * (l - 1)
+        col = 192 * (l - 1)
         k_raw = []
-        wait("s", fa[l - 1], k_off[l], k_wz, k_wz2, k_y[l - 1])
+        wait("s", fa[l - 1], k_off[l], k_wz, k_wz2, k_y[l - 1], *([k_m[l - 1]] if l > 1 else []))
         for a, e in CH:
             k_raw.append(copy(T.raw[:, a - NV:e - NV], win.indirect(T.offf[:, col + a // 16:col + e // 16])))
-        wait("v", fa[l - 1], k_off[l], k_wz, k_wz2, k_cst[l], k_y[l - 1])
-        if l < 4:
-            k_p = [done("v", v.tensor_tensor(T.prod[:, 0:NV], win.indirect(T.offf[:, col:col + NV // 16]), T.valf[:, base:base + NV], MUL))]
-        else:
-            k_p = [done("v", v.tensor_tensor(blk[0], win.indirect(T.offf[:, col:col + M // 16]), T.valf[:, base:base + M], MUL))]
-            done("v", v.tensor_tensor(T.prod[:, M:NV], win.indirect(T.offf[:, col + M // 16:col + NV // 16]), T.valf[:, base + M:base + NV], MUL))
-
-        def product(i):
-            a, e = CH[i]
-            wait("v", k_raw[i], k_fac[l])
-            k_p.append(done("v", v.tensor_tensor(T.prod[:, a:e], T.raw[:, a - NV:e - NV], T.fac[:, a - NV:e - NV], MUL)))
-
+        wait("v", fa[l - 1], k_off[l], k_wz, k_wz2, k_f[l], k_y[l - 1])
+        made = []
         cs = [T.bsh[:, l * SH:(l + 1) * SH], T.c0[:, :], T.c1[:, :], T.c2[:, :], T.sh[:, l * SH:(l + 1) * SH]] if l < 4 else None
         k_c = [k_bsh]
 
-        def shown(e):
-            wait("v", k_sl, k_p[e], k_c[-1])
-            k_c.append(done("v", v.tensor_tensor(cs[e + 1], blk[e].indirect(sl_cols(l, 0, 9)), cs[e], ADD)))
+        def k_p(e):
+            return min(t for t in made if t[0] >= (e + 1) * M)[1]
 
-        product(0)
-        if l < 4:
-            shown(0)
-        product(1)
-        if l < 4:
+        def shown(lag):
+            while l < 4 and len(k_c) < 5 and len(made) > lag and made[-1 - lag][0] >= len(k_c) * M:
+                e = len(k_c) - 1
+                wait("v", k_sl, k_p(e), k_c[-1])
+                k_c.append(done("v", v.tensor_tensor(cs[e + 1], blk[e].indirect(sl_cols(l, 0, 9)), cs[e], SUB if e < 2 else ADD)))
+
+        made.append((M, done("v", v.tensor_tensor(blk[0], win.indirect(T.offf[:, col:col + M // 16]), T.valf[:, M * (l - 1):M * l], MUL))))
+        for i, (a, e) in enumerate(CH):
+            wait("v", k_raw[i], k_fac[l])
+            made.append((e, done("v", v.tensor_tensor(T.prod[:, a:e], T.raw[:, a - NV:e - NV], T.fac[:, a:e], MUL))))
             shown(1)
-        product(2)
-        k_m[l] = k_p[3]
+        k_m[l] = made[-1][1]
+        shown(0)
         if l < 4:
-            shown(2)
-            shown(3)
             wait("g", k_c[-1])
             send(l, T.sh, T.w, R, True)
-            g_zero(l)
 
-        def tensor_add(a, e, i, last):
-            wait("t", k_p[i], k_idf)
-            return done("t", g.tensor.matmul(T.acc[:, a:e], T.idf[:, :], T.prod[:, i * M + a:i * M + e], False, last))
+        def tensor_add(a, e, i, stop):
+            wait("t", k_p(i), k_idf, k_nid)
+            return done("t", g.tensor.matmul(T.acc[:, a:e], (T.idf if i else T.nid)[:, :], T.prod[:, i * M + a:i * M + e], False, stop))
 
-        k_acc0 = tensor_add(0, PB, 0, True)
-        tensor_add(PB, M, 0, False)
-        k_acc1 = tensor_add(PB, M, 1, True)
+        k_acc = {}
+        for i in range(3):
+            for j, (a, e) in enumerate(banks):
+                if i < TA[l - 1][j]:
+                    k_acc[j] = tensor_add(a, e, i, i == TA[l - 1][j] - 1)
+        wait("y", fa[l - 1])
+        snapshot(l - 1)
         if l < 4:
-            wait("y", fa[l - 1])
-            ld_v("y", l + 1)
+            if l > 1:
+                ld_v("y", l + 1)
             ld_b("y", l + 1)
-            ld_e("y", l + 1)
-            wait("s", k_bz0)
-            a = RS + M * (l - 1)
-            k_bz.append(copy(T.bk[:, a:a + M], T.bk[:, 0:M]))
-            prep_stage(l + 1)
             if l < 3:
-                k_bsh = shown_b(l + 1)
+                wait("y", left[l])
+                ld_f("y", l + 2)
+        scatter(l)
+        if l < 3:
+            k_bsh = shown_b(l + 1)
 
         def vector_add(a, e, i, *need):
-            wait("v", k_p[i], *need)
+            wait("v", k_p(i), *need)
             out = T.acc[:, a:e] if i < 3 else T.w[:, l * M + a:l * M + e]
             return done("v", v.tensor_tensor(out, T.acc[:, a:e], T.prod[:, i * M + a:i * M + e], ADD))
 
-        k_h = [k_acc0, k_acc0]
+        if l == 3:
+            wait("v", ("ini", 32))
         for i in range(1, 4):
-            for h in range(2):
-                k_h[h] = vector_add(h * PB // 2, (h + 1) * PB // 2, i, k_h[h])
-        k_acc1 = vector_add(PB, M, 2, k_acc1)
-        k_a3[l] = k_y[l] = vector_add(PB, M, 3, k_acc1)
+            for j, (a, e) in enumerate(banks):
+                if i >= TA[l - 1][j]:
+                    k_acc[j] = k_a3[l] = k_y[l] = vector_add(a, e, i, k_acc[j])
         if l < 4:
             wait("t", k_m[l])
-            prep_fac(l + 1)
+            k_fac[l + 1] = factors(l + 1, NV if l < 3 else PB, K)
             prep_acc(l + 1)
             lists(l + 1)
-        else:
-            wait("s", k_m[4])
-            copy_fac(4)
-    slots(4)
+            positions(POS[l + 1], POS[l], T.fac)
+            if l == 3:
+                wait("t", *k_pos.values())
+                k_f4 = factors(4, 0, PB)
+            if l == 3:
+                convert(3)
+
+    SB = M - VA
+
+    def start_acc(l, need):
+        wait("t", need)
+        bank = PB * (l % 2)
+        done("t", g.tensor.matmul(T.acc[:, bank:bank + SB], T.idf[:, :], T.w[:, l * M + VA:(l + 1) * M], True, False))
 
     k_z = k_a3[4]
+    start_acc(3, k_z)
+    k_bf = k_f4
     stores = 0
     for l in range(4, -1, -1):
         if l < 4:
-            a = RS + 4 * SH * l
-            x = done("v", v.tensor_tensor(T.u1[:, :], T.bk[:, a:a + 4 * SH:2], T.bk[:, a + 1:a + 4 * SH:2], ADD))
-            wait("v", x)
-            k_rs = done("v", v.tensor_tensor(T.rsum[:, l * SH:(l + 1) * SH], T.u1[:, 0:2 * SH:2], T.u1[:, 1:2 * SH:2], ADD))
+            win = T.pr[:, 0:PAD + K * (4 - l)]
+            wl = T.w[:, M * l:M * (l + 1)]
+            acc = T.acc[:, PB * (l % 2):PB * (l % 2) + SB]
+            wait("s", k_pr, k_list[l][1], k_pad)
+            if FOLD == 4:
+                wait("s", left[-1])
+                wait("g", copy(T.rsum[:, 2 * SH:4 * SH], win.indirect(T.offr[:, 36 * l:36 * l + 18])))
+            k_raw = [copy(T.raw[:, s * SB:(s + 1) * SB], win.indirect(T.offo[:, 192 * l + 48 * s + VA // 16:192 * l + 48 * (s + 1)]))
+                     for s in range(4)]
+            wait("v", k_pr, k_list[l][0], k_pad)
+            if FOLD == 4:
+                wait("v", left[-1])
+                k_rs = done("v", v.tensor_copy(T.rsum[:, 0:2 * SH], win.indirect(T.offr[:, 36 * l + 18:36 * l + 36])))
+            else:
+                x = done("v", v.tensor_copy(T.u1[:, :], win.indirect(T.offr[:, 36 * l:36 * l + 18])))
+                wait("v", x, left[-1])
+                k_rs = done("v", v.tensor_tensor(T.rsum[:, 0:2 * SH], win.indirect(T.offr[:, 36 * l + 18:36 * l + 36]), T.u1[:, :], ADD))
             wait("g", k_rs)
             send(l, T.rsum, T.rc, 0, False)
-            wait("t", k_sc, k_cst[4])
-            for s in range(4):
-                k_t = done("t", g.tensor.matmul(T.stg[:, 0:TC], T.idf[:, :], T.bk[:, K * l + 4 * VC + s:K * (l + 1):4], s == 0, s == 3))
-            k_h = [k_yc, k_yc]
-            for s in range(4):
-                for h, (a, e) in enumerate(((0, VC // 2), (VC // 2, VC))):
-                    wait("v", k_h[h])
-                    out = T.acc[:, a:e] if s < 3 else T.w[:, l * M + a:l * M + e]
-                    k_h[h] = done("v", v.tensor_tensor(out, T.acc[:, a:e], T.bk[:, K * l + 4 * a + s:K * l + 4 * e:4], ADD))
+            snapshot(7 - l, *([left[-1]] if AFTER else []))
+            early = set(k_snap)
+            if 8 - l < len(SLOTS):
+                scatter(8 - l)
+            wait("t", k_pr)
             if l > 0:
-                slots(l)
-            wait("v", k_t)
-            tail = T.w[:, l * M + VC:(l + 1) * M]
-            x = done("v", v.tensor_tensor(tail, T.stg[:, 0:TC], tail, ADD))
+                factors(l, 0, PB)
+            for s in range(TB):
+                wait("t", k_raw[s])
+                k_t = done("t", g.tensor.matmul(acc, T.idf[:, :], T.raw[:, s * SB:(s + 1) * SB], False, s == TB - 1))
+            if l > 0:
+                k_bf = factors(l, PB, K)
+                start_acc(l - 1, k_z)
+            wait("v", k_list[l][1])
+            k_h = [k_z, k_z]
+            for s in range(4):
+                for h, (a, e) in enumerate(((0, VA // 2), (VA // 2, VA))):
+                    wait("v", k_h[h])
+                    src = wl[:, a:e] if False else (T.w[:, M * l + a:M * l + e] if s == 0 else T.prod[:, M * (s - 1) + a:M * (s - 1) + e])
+                    out = T.w[:, M * l + a:M * l + e] if s == 3 else T.prod[:, M * s + a:M * s + e]
+                    c = 192 * l + 48 * s
+                    k_h[h] = done("v", v.tensor_tensor(out, win.indirect(T.offo[:, c + a // 16:c + e // 16]), src, ADD))
+            if l - 1 in early:
+                convert(l - 1)
+            x = k_t
+            for s in range(TB, 4):
+                wait("v", x, k_raw[s])
+                x = done("v", v.tensor_tensor(acc if s < 3 else T.w[:, M * l + VA:M * (l + 1)], acc, T.raw[:, s * SB:(s + 1) * SB], ADD))
             wait("v", x)
             ds = sorted(range(3), key=lambda d: topo.chip(cores[(rank + 1 + d) % N]) != topo.chip(core))
-            win = T.w[:, M * l:M * (l + 1)]
             for d in ds:
                 a = (l * 3 + d) * S
                 wait("v", ba[l, d])
-                x = done("v", v.tensor_tensor(T.tmp[:, :], win.indirect(sl_cols(l, d, 3)), T.rc[:, a:a + S], ADD))
+                x = done("v", v.tensor_tensor(T.tmp[:, :], wl.indirect(sl_cols(l, d, 3)), T.rc[:, a:a + S], ADD))
                 wait("v", x)
-                k_z = done("v", v.tensor_copy(win.indirect(sl_cols(l, d, 3)), T.tmp[:, :]))
+                k_z = done("v", v.tensor_copy(wl.indirect(sl_cols(l, d, 3)), T.tmp[:, :]))
                 wait("v", k_z)
         zl = T.w[:, l * M:(l + 1) * M]
         wait("y", k_z)
         g.sync.dma_start(T.z[:, l * M:(l + 1) * M], zl).then_inc(T.sem["st"], 16)
         stores += 16
         if l > 0:
-            wait("s", k_z)
-            copy(T.zrep[:, 0:M], zl)
-            k_rep = copy(T.zrep[:, M:2 * M], zl)
-            k_yc = copy(T.acc[:, 0:VC], T.w[:, (l - 1) * M:(l - 1) * M + VC])
-            base, col = K * (l - 1), 192 * (l - 1)
-            bwin = T.bk[:, 0:RS + 4 * SH * l]
-            for a, e, src, need in ((0, M, zl, [k_z, k_offb[l], k_cst[4]] + k_bz), (M, 2 * M, zl, [k_cfac[l]]),
-                                    (2 * M, K, T.zrep[:, :], [k_rep])):
-                wait("v", *need)
-                k_sc = done("v", v.tensor_tensor(bwin.indirect(T.offb[:, col + a // 16:col + e // 16]), src, T.valf[:, base + a:base + e], MUL))
-                wait("v", k_sc)
-            if l > 1:
-                wait("t", k_cfac[l])
-                prep_fac(l - 1)
-                wait("s", k_fac[l - 1])
-                copy_fac(l - 1)
+            wait("v", k_z, k_bf, k_scat[l])
+            base = PAD + K * (4 - l)
+            for e in range(4):
+                k_pr = done("v", v.tensor_tensor(T.pr[:, base + e * M:base + (e + 1) * M], zl, T.fac[:, e * M:(e + 1) * M], MUL))
+            if l - 1 not in k_list:
+                convert(l - 1)
     g.sync.wait_ge(T.sem["st"], stores)
-    g.wait_ge(T.sem["loc"], 8 * local_each)
+    wait("g", *left)
     wait("v", ("ss", count["ss"]), ("ts", count["ts"]), ("gs", count["gs"]))

@@ -6,20 +6,31 @@ R, SH = LV * M, (N - 1) * S
 K = 4 * M
 QN = (R + 4 * SH) // 16
 PB = 512
-PAD, LIFT = 8, 32
+EARLY = ()
+DEFER = (1, 2, 3)
+XM = 192
+PAD, LIFT = 16, 752
 NV = M
 CH = ((768, 1536), (1536, 2304), (2304, 2816), (2816, 3072))
-VA = 384
-COPIER = "svvv"
-POS = (768, 192, 96, 0, 0)
-AFTER = False
-TA = ((1, 2), (1, 2), (1, 2), (1, 2))
-TB = 2
+VAS = (512, 544, 544, 544)
+SPLIT = True
+QM, AM = 1536, 1560
+CUT = 256
+SQ = 9
+TIMES = (-64.0, 63.0, 1365 / 65536)
+TA = ((1, 1), (1, 2), (1, 2), (1, 2))
+TBS = (256, 224, 224, 224)
+HALVES = True
+XA, NX = 1152, 0
+FIRST = True
+RS = 36
+PV = 128
+B1 = True
 FOLD = 4
 WIDE = 8
-SLOTS = (0, 1792, 1920, 2048, 2432, 2048, 2048)
-SNAPS = {2: 3, 4: 2, 5: 1, 6: 0}
-IOTAS = (0, 1792, 1920, 2048, 4480, 2048)
+SLOTS = (0, 1280, 1792, 1536, 2304, 2304, 1920, 1152)
+SNAPS = {2: 3, 4: 2, 5: 1, 7: 0}
+IOTAS = SLOTS[:4] + (SLOTS[4] + SLOTS[5],) + SLOTS[6:]
 PIECE = 1024
 
 SCRATCH = {
@@ -28,39 +39,43 @@ SCRATCH = {
     "invo": ("sbuf", [128, 768], "float32"),
     "invr": ("sbuf", [128, 4, 4, 48], "float32"),
     "pr": ("sbuf", [128, PAD + 4 * K], "float32"),
-    "valf": ("sbuf", [128, K], "bfloat16"),
+    "valf": ("sbuf", [128, PAD + 4 * K], "bfloat16"),
+    "m768": ("sbuf", [128, 128], "bfloat16"),
+    "xt": ("sbuf", [128, 72], "bfloat16"),
+    "xn": ("sbuf", [128, 36], "float32"),
+    "offx": ("sbuf", [128, 160], "uint16"),
+    "vsh": ("sbuf", [128, 4 * SH], "float32"),
     "nid": ("sbuf", [128, 128], "float32"),
+    "first": ("sbuf", [128, 36], "int32"),
     "bsb": ("sbuf", [128, R], "bfloat16"),
-    "vsb": ("sbuf", [128, 4 * K], "bfloat16"),
+    "vsb": ("sbuf", [128, 2 * K], "bfloat16"),
     "ents": ("sbuf", [128, 768], "int32"),
-    "e1": ("sbuf", [128, 768], "int32"),
-    "e2": ("sbuf", [128, 768], "int32"),
+    "q16": ("sbuf", [128, 768], "float16"),
+    "a16": ("sbuf", [128, 768], "float16"),
+    "times": ("sbuf", [128, 384], "float16"),
     "offf": ("sbuf", [128, 768], "uint16"),
     "pos": ("sbuf", [128, 768], "uint16"),
     "offo": ("sbuf", [128, 768], "uint16"),
-    "offr": ("sbuf", [128, 144], "uint16"),
+    "offr": ("sbuf", [128, 160], "uint16"),
     "slr": ("sbuf", [128, 36], "int32"),
     "slq": ("sbuf", [128, 36], "int32"),
     "sla": ("sbuf", [128, 40], "uint16"),
     "slb": ("sbuf", [128, 40], "uint16"),
     "prod": ("sbuf", [128, K], "float32"),
-    "raw": ("sbuf", [128, max(K - NV, 4 * (M - VA))], "float32"),
+    "raw": ("sbuf", [128, K - NV], "float32"),
     "bsh": ("sbuf", [128, 4 * SH], "float32"),
     "c0": ("sbuf", [128, SH], "float32"),
     "c1": ("sbuf", [128, SH], "float32"),
     "c2": ("sbuf", [128, SH], "float32"),
-    "sh": ("sbuf", [128, 4 * SH], "float32"),
+    "sh": ("sbuf", [128, 3 * SH], "float32"),
     "rsum": ("sbuf", [128, 4 * SH], "float32"),
     "rc": ("sbuf", [128, 4 * SH], "float32"),
-    "u1": ("sbuf", [128, 2 * SH], "float32"),
-    "u2": ("sbuf", [128, 2 * SH], "float32"),
     "tmp": ("sbuf", [128, S], "float32"),
     "negb": ("sbuf", [128, 128], "bfloat16"),
     "sel0": ("sbuf", [128, 128], "bfloat16"),
     "sel": ("sbuf", [128, 128], "bfloat16"),
     "oneb": ("sbuf", [128, 128], "bfloat16"),
     "idb": ("sbuf", [128, 128], "bfloat16"),
-    "onef": ("sbuf", [128, 128], "float32"),
     "idf": ("sbuf", [128, 128], "float32"),
     "acc": ("psum", [128, 2 * PB], "float32"),
     "fac": ("psum", [128, 6 * PB], "float32"),
@@ -68,7 +83,7 @@ SCRATCH = {
 SEMAPHORES = (["vs", "ss", "ts", "gs", "st", "ldsl", "ini"] + ["loc%d" % i for i in range(8)]
               + ["snap%d" % i for i in SNAPS]
               + ["ldb%d" % l for l in range(5)] + ["lde"]
-              + ["ldv%d" % l for l in range(1, 5)] + ["ldf%d" % l for l in range(3, 5)] + ["fa%d" % h for h in range(4)]
+              + ["ldv1", "ldv3", "ldf2", "ldf3", "ldf4"] + ["ldg%d" % (h + 1) for h in EARLY] + ["fa%d" % h for h in range(4)]
               + ["ba%d_%d" % (h, d) for h in range(4) for d in range(3)])
 
 
@@ -89,7 +104,7 @@ def engine_plan(src, dsts, topo, most):
 def pieces(a, e):
     out = []
     while a < e:
-        x = min(e, a + PIECE, (a // K + 1) * K)
+        x = min(e, (a // K + 1) * K)
         out.append((a, x))
         a = x
     return out
@@ -101,6 +116,7 @@ def rank_program(g, core, T, topo):
         return
     ADD, SUB, MUL = AluOpType.add, AluOpType.subtract, AluOpType.mult
     COPY, SILU = ActivationFunctionType.Copy, ActivationFunctionType.Silu
+    IDENT = COPY
     cores = list(T.cores)
     q = {"v": g.vector, "s": g.scalar, "t": g.tensor, "g": g, "y": g.sync}
     own = {"v": "vs", "s": "ss", "t": "ts", "g": "gs"}
@@ -127,87 +143,126 @@ def rank_program(g, core, T, topo):
         return done("s", g.scalar.activation(out, in_, COPY))
 
     others = [c for c in cores if c != core]
-    most = {True: 4, False: WIDE}
-    plans = {f: engine_plan(core, others, topo, most[f]) for f in most}
-    arrive = {f: {c: len(engine_plan(c, [x for x in cores if x != c], topo, most[f])[core]) for c in others} for f in most}
+
+    def calls(r, forward):
+        dsts = {cores[(r + 1 + d) % N] if forward else cores[(r - 1 - d) % N]: d for d in range(3)}
+        far = [c for c in dsts if topo.chip(c) != topo.chip(cores[r])]
+        sets = [list(dsts)] if forward or not SPLIT else [[c for c in dsts if c != far[-1]], far[-1:]]
+        plans = [engine_plan(cores[r], x, topo, 4 if forward else WIDE) for x in sets]
+        return [[(dsts[c], c, plan[c]) for c in plan] for plan in plans]
+
+    arrive = {f: {cores[r]: len(e) for r in range(N) for call in calls(r, f) for d, c, e in call if c == core} for f in (True, False)}
     left = []
 
     def send(h, src, dst, dst_base, forward):
-        tr = []
-        plan = plans[forward]
-        local_each = sum(len(e) for e in plan.values())
-        for d in range(3):
-            c = cores[(rank + 1 + d) % N] if forward else cores[(rank - 1 - d) % N]
-            rid, pid = topo.addr(c)[:2]
-            a = (h * 3 + d) * S
-            m = sum(1 << e for e in plan[c])
-            sem = T.sem["fa%d" % h] if forward else T.sem["ba%d_%d" % (h, d)]
-            srcs = [src[:, a:a + S]] if forward else [src[:, s * SH + d * S:s * SH + (d + 1) * S] for s in range(FOLD)]
-            tr.append(RemoteDMATransfer(dst_ids=[DstId(rid=rid, pnc=pid)], dma_engine_mask=m, remote_sem=sem,
-                                        srcs=srcs, dsts=[dst[:, dst_base + a:dst_base + a + S]],
-                                        alu_op=0 if forward else 1))
-        name = "loc%d" % len(left)
-        g.remote_dma_fused(tr, local_sem=T.sem[name])
+        name, local_each = "loc%d" % len(left), 0
+        for call in calls(rank, forward):
+            tr = []
+            for d, c, engines in call:
+                rid, pid = topo.addr(c)[:2]
+                a = (h * 3 + d) * S
+                sem = T.sem["fa%d" % h] if forward else T.sem["ba%d_%d" % (h, d)]
+                n = 4 if not forward else 3 if h else 1
+                srcs = [src[:, s * SH + d * S:s * SH + (d + 1) * S] for s in range(n)]
+                tr.append(RemoteDMATransfer(dst_ids=[DstId(rid=rid, pnc=pid)], dma_engine_mask=sum(1 << e for e in engines),
+                                            remote_sem=sem, srcs=srcs, dsts=[dst[:, dst_base + a:dst_base + a + S]],
+                                            alu_op=1 if n > 1 else 0))
+                local_each += len(engines)
+            g.remote_dma_fused(tr, local_sem=T.sem[name])
         left.append((name, local_each))
-        lay(len(left))
+        if len(left) > 1:
+            lay(len(left))
 
     fa = {h: ("fa%d" % h, sum(arrive[True].values())) for h in range(4)}
     ba = {(h, d): ("ba%d_%d" % (h, d), arrive[False][cores[(rank + 1 + d) % N]]) for h in range(4) for d in range(3)}
 
-    laid, k_pos, k_snap, k_list, k_scat = [], {}, {}, {}, {}
-    last = {"scat": [], "conv": []}
+    laid, k_pos, k_snap, k_list, k_free = [], {}, {}, {}, {}
+    last = {"scat": []}
+    late = sum(SLOTS[:7])
+
+    def numbers(x, e):
+        return T.pr[:, PAD + x:PAD + e] if x < late else T.prod[:, x - 3 * K:e - 3 * K]
 
     def lay(i):
         if i < len(IOTAS):
             a = sum(IOTAS[:i])
-            for x, e in pieces(a, a + IOTAS[i]):
-                laid.append((e, done("g", g.iota(T.pr[:, PAD + x:PAD + e], [[1, e - x]], PAD + x + LIFT, 0,
+            for x, e in pieces(a, min(late, a + IOTAS[i])) + pieces(max(a, late), a + IOTAS[i]):
+                laid.append((e, done("g", g.iota(numbers(x, e), [[1, e - x]], PAD + x + LIFT, 0,
                                                  allow_small_or_imprecise_dtypes=True))))
 
-    def positions(a, b, psum):
-        if a < b:
-            levels = range(a // 192 + 1, (b - 1) // 192 + 2)
-            e, e1, e2 = T.ents[:, a:b], T.e1[:, a:b], T.e2[:, a:b]
-            y = psum[:, 0:b - a]
-            wait("v", *[k_ent[l] for l in levels])
-            x1 = done("v", v.tensor_scalar(e1, e, 63, None, AluOpType.bitwise_and))
-            x2 = done("v", v.tensor_scalar(e2, e, 1.0 / K, 0.5 / K - 0.5, MUL, ADD))
-            wait("v", x1)
-            x1 = done("v", v.tensor_scalar(y, e1, K - 1, None, MUL))
-            wait("v", x2)
-            x2 = done("v", v.tensor_scalar(e2, e2, 63 * K, None, MUL))
-            wait("v", x1)
-            x1 = done("v", v.tensor_tensor(y, y, e, ADD))
-            wait("v", x1, x2)
-            x1 = done("v", v.tensor_tensor(e1, y, e2, ADD))
-            wait("v", x1)
-            x1 = done("v", v.tensor_scalar(T.pos[:, a:b], e1, 1.0 / 64, None, MUL))
-            k_pos.update({l: x1 for l in levels})
+    def rounded(a, e):
+        wait("v", ("lde", 16))
+        done("v", v.tensor_scalar(T.q16[:, a:e], T.ents[:, a:e], 1.0 / 64, QM - 0.5 + 0.5 / 64, MUL, ADD))
+        return done("v", v.tensor_scalar(T.a16[:, a:e], T.ents[:, a:e], 1.0 / K, AM - 0.5 + 0.5 / K, MUL, ADD))
 
-    def scatter(i):
-        a = sum(SLOTS[:i])
+    def multiples(a, e, psum, *need):
+        wait("t", k_times, *need)
+        for i, src in enumerate((T.q16, T.a16, T.q16)):
+            k = done("t", g.tensor.matmul(psum, T.times[:, 128 * i:128 * i + 128], src[:, a:e], i == 0, i == 2))
+        return k
+
+    def positions(a, e, psum, need, between):
+        wait("v", need)
+        x = done("v", v.tensor_tensor(psum, psum, T.ents[:, a:e], ADD))
+        between()
+        wait("v", x)
+        x = done("v", v.tensor_scalar(T.pos[:, a:e], psum, 64 * QM - 63 * AM - QM * TIMES[2], 48, ADD, MUL))
+        k_pos.update({l: x for l in range(a // 192 + 1, (e - 1) // 192 + 2)})
+
+    def scatter(i, between=None):
+        a, out = sum(SLOTS[:i]), None
         for x, e in pieces(a, a + SLOTS[i]):
+            if between and x > a:
+                out = between()
             l = 4 - x // K
             col = 192 * (l - 1) + (x % K) // 16
-            wait("s", ("ini", 32), k_pos[l], min(t for t in laid if t[0] >= e)[1], *last["scat"])
-            k_scat[l] = done("s", g.scalar.activation(T.inv[:, :].indirect(T.pos[:, col:col + (e - x) // 16]),
-                                                      T.pr[:, PAD + x:PAD + e], SILU))
-            last["scat"] = [k_scat[l]]
+            wait("s", ("ini", 16), k_pos[l], min(t for t in laid if t[0] >= e)[1], *last["scat"])
+            k = done("s", g.scalar.activation(T.inv[:, :].indirect(T.pos[:, col:col + (e - x) // 16]), numbers(x, e), SILU))
+            last["scat"] = [k]
+            if i < 7:
+                k_free[l] = k
+        return out
+
+    def rounded_columns(h):
+        wait("s", k_snap[h])
+        src = T.invr[:, h, :, 9 * h:9 * h + 9]
+        copy(T.xn[:, :], src)
+        done("s", g.scalar.activation(T.xt[:, 0:36], src, IDENT, bias=XM - 0.5 + 0.5 / M, scale=1.0 / M))
+        return done("s", g.scalar.activation(T.xt[:, 36:72], src, IDENT, bias=XM + 0.25 + 0.5 / K, scale=1.0 / K))
+
+    def unknowns(h, need):
+        wait("t", need, k_m768)
+        for i in range(2):
+            done("t", g.tensor.matmul(T.fac[:, 5 * PB:5 * PB + 36], T.m768[:, :], T.xt[:, 36 * i:36 * i + 36], i == 0, False))
+        return done("t", g.tensor.matmul(T.fac[:, 5 * PB:5 * PB + 36], T.idf[:, :], T.xn[:, :], False, True))
+
+    def unknown_list(h, need):
+        wait("v", need)
+        k = done("v", v.tensor_scalar(T.offx[:, 40 * h:40 * h + 36], T.fac[:, 5 * PB:5 * PB + 36], R + 2 * M * XM, None, ADD))
+        wait("t", k)
+        return k
+
+    def slot_factors(h):
+        wait("s", k_list[h, 0], k_vpad, ("ldg%d" % (h + 1), 256), ("ldf%d" % (h + 1), 256))
+        return done("s", g.scalar.activation(T.vsh[:, :], T.valf[:, 0:PAD + K * (4 - h)].indirect(T.offr[:, 40 * h:40 * h + 36]),
+                                             COPY, scale=-1.0))
 
     def snapshot(i, *need):
         if i in SNAPS:
             h = SNAPS[i]
-            wait("y", *(last["scat"] + list(need)))
-            g.sync.dma_start(T.invr[:, h, :, :], T.inv[0:128:16, 5 * K:6 * K]).then_inc(T.sem["snap%d" % i], 16)
-            g.sync.dma_start(T.invo[:, 192 * h:192 * h + 192], T.inv[0:128:16, h * K:(h + 1) * K]).then_inc(T.sem["snap%d" % i], 16)
+            k = "y" if i < SQ else "s"
+            wait(k, *(last["scat"] + list(need)))
+            load(k, "snap%d" % i, T.invr[:, h, :, :], T.inv[0:128:16, 5 * K:6 * K])
+            load(k, "snap%d" % i, T.invo[:, 192 * h:192 * h + 192], T.inv[0:128:16, h * K:(h + 1) * K])
             k_snap[h] = ("snap%d" % i, 32)
             last["scat"] = [k_snap[h]]
 
-    def convert(h):
+    def convert(h, parts=(0, 1)):
         wait("v", k_snap[h])
-        x = done("v", v.tensor_scalar(T.offr[:, 36 * h:36 * h + 36], T.invr[:, h, :, 9 * h:9 * h + 9], -LIFT, None, ADD))
-        y = done("v", v.tensor_scalar(T.offo[:, 192 * h:192 * h + 192], T.invo[:, 192 * h:192 * h + 192], -LIFT, None, ADD))
-        k_list[h] = (x, y)
+        for i in parts:
+            out, in_ = ((T.offr[:, 40 * h:40 * h + 36], T.invr[:, h, :, 9 * h:9 * h + 9]),
+                        (T.offo[:, 192 * h:192 * h + 192], T.invo[:, 192 * h:192 * h + 192]))[i]
+            k_list[h, i] = done("v", v.tensor_scalar(out, in_, -LIFT, None, ADD))
 
     def load(k, name, out, in_):
         q[k].dma_start(out, in_).then_inc(T.sem[name], 16)
@@ -217,41 +272,56 @@ def rank_program(g, core, T, topo):
 
     def ld_v(k, l):
         a = K * (l - 1)
-        load(k, "ldv%d" % l, T.vsb[0:8, a:a + K], T.val[:, a:a + K])
+        load(k, "ldv%d" % l, T.vsb[16 * l - 16:16 * l - 8, :], T.val[:, a:a + 2 * K])
+
+    k_v = {l: ("ldv%d" % (l - (l + 1) % 2), 16) for l in range(1, 5)}
+
+    def vf(l, e):
+        return PAD + K * (4 - l) + M * e
+
+    def spread(k, name, l, a, e):
+        for c in range(16):
+            x = M - PB if l == 4 else 0
+            load(k, name, T.valf[c:128:16, vf(l, a) - x:vf(l, e)], T.val[:, K * (l - 1) + M * a - x:K * (l - 1) + M * e])
 
     def ld_f(k, l):
-        for c in range(16):
-            load(k, "ldf%d" % l, T.valf[c:128:16, M * (l - 1):M * l], T.val[:, K * (l - 1):K * (l - 1) + M])
+        spread(k, "ldf%d" % l, l, *{2: (2, 3), 3: (2 if 3 in DEFER else 3, 4), 4: (3, 4)}[l])
+
+    def ld_g(k, l):
+        spread(k, "ldg%d" % l, l, 0, 3 if l == 4 else 2)
 
     load("s", "ldsl", T.slr[:, :], T.sl[:, :])
     ld_b("y", 0)
     wait("y", ("ldsl", 16))
     load("y", "lde", T.ents[:, :], T.ent[:, :])
     k_ent = {l: ("lde", 16) for l in range(1, 5)}
-    ld_v("y", 1)
-    ld_v("y", 2)
-    ld_b("y", 1)
-
-    def clear():
-        wait("y", k_wz)
-        load("y", "ini", T.inv[0:128:16, 0:4 * K], T.w[:, 2304:2304 + M])
-        load("y", "ini", T.inv[0:128:16, 5 * K:6 * K], T.w[:, 2304:2304 + 192])
 
     v = g.vector
     k_neg = done("v", v.memset(T.negb[:, :], -1.0))
-    k_wz = done("v", v.memset(T.w[:, 2304:3840], 0.0))
     k_oneb = done("v", v.memset(T.oneb[:, :], 1.0))
-    k_onef = done("v", v.memset(T.onef[:, :], 1.0))
+    k_wz = done("v", v.memset(T.w[:, 2304:3840], 0.0))
     k_pad = done("v", v.memset(T.pr[:, 0:PAD], 0.0))
-    lay(0)
+    k_first = done("g", g.iota(T.first[:, :], [[M, 4], [0, 9]], 0, 0))
     wait("g", k_neg)
-    x = done("g", g.affine_select(T.sel0[0:8, :], T.negb[0:8, :], [[1, 128]], AluOpType.is_ge, 0.0, 0, -16))
-    wait("g", x)
-    k_sel = done("g", g.affine_select(T.sel[0:8, :], T.sel0[0:8, :], [[-1, 128]], AluOpType.is_ge, 0.0, 15, 16))
+
+    def selection(p):
+        wait("g", done("g", g.affine_select(T.sel0[p:p + 8, :], T.negb[p:p + 8, :], [[1, 128]], AluOpType.is_ge, 0.0, 0, -16)))
+        return done("g", g.affine_select(T.sel[p:p + 8, :], T.sel0[p:p + 8, :], [[-1, 128]], AluOpType.is_ge, 0.0, 15, 16))
+
+    k_sel = selection(0)
     wait("g", k_oneb)
     k_idb = done("g", g.affine_select(T.idb[:, :], T.oneb[:, :], [[-1, 128]], AluOpType.is_equal, 0.0, 0, 1))
+    lay(0)
     wait("s", k_wz)
-    k_wz2 = copy(T.w[:, 768:2304], T.w[:, 2304:3840])
+    k_wz2 = done("s", g.scalar.activation(T.w[:, 768:2304], T.w[:, 2304:3840], SILU))
+    ld_v("y", 1)
+    if B1:
+        ld_b("y", 1)
+
+    def clear():
+        wait("y", k_wz)
+        load("y", "ini", T.inv[0:128:16, :], T.w[:, 2304:2304 + 6 * K // 16])
+
     if SLOTS[0]:
         clear()
 
@@ -262,15 +332,27 @@ def rank_program(g, core, T, topo):
         c = h * 9 + d * 3
         return T.sla[:, c:c + n] if c % 2 == 0 else T.slb[:, c + 1:c + 1 + n]
 
+    wait("v", k_first)
+    k_slq = done("v", v.tensor_tensor(T.slq[:, :], T.slr[:, :], T.first[:, :], SUB))
     wait("v", ("ldb0", 16), k_sl)
     k_sh = done("v", v.tensor_copy(T.sh[:, 0:SH], T.bsb[:, 0:M].indirect(sl_cols(0, 0, 9))))
-    wait("g", k_onef)
-    k_idf = done("g", g.affine_select(T.idf[:, :], T.onef[:, :], [[-1, 128]], AluOpType.is_equal, 0.0, 0, 1))
     wait("g", k_sh)
     send(0, T.sh, T.w, R, True)
+    wait("g", k_wz, k_oneb)
+    k_idf = done("g", g.affine_select(T.idf[:, :], T.w[:, 3584:3712], [[-1, 128]], AluOpType.not_equal, 1.0, 0, 1))
+    k_nid = done("g", g.affine_select(T.nid[:, :], T.w[:, 3584:3712], [[-1, 128]], AluOpType.not_equal, -1.0, 0, 1))
+    lay(1)
+    wait("g", laid[-1][1])
+    k_sel2 = selection(32)
+    wait("g", k_sel2)
+    wait("y", left[0])
+    if not B1:
+        ld_b("y", 1)
     if not SLOTS[0]:
-        wait("y", left[0])
         clear()
+    ld_b("y", 2)
+    if 2 in DEFER:
+        ld_f("y", 2)
 
     wait("s", ("ldb0", 16))
     k_y = {0: copy(T.w[:, 0:M], T.bsb[:, 0:M])}
@@ -279,28 +361,31 @@ def rank_program(g, core, T, topo):
 
     def lists(l):
         a = 192 * (l - 1)
-        wait("v", ("lde", 16))
+        wait("v", k_ent[l])
         k_off[l] = done("v", v.tensor_scalar(T.offf[:, a:a + 192], T.ents[:, a:a + 192], 0.25, -0.375, MUL, ADD))
 
-    for h in range(1, 4):
-        x = done("v", v.tensor_scalar(T.slq[:, 9 * h:9 * h + 9], T.slr[:, 9 * h:9 * h + 9], -M * h, None, ADD))
-    done("v", v.tensor_copy(T.slb[:, 1:10], T.slr[:, 0:9]))
-    wait("v", x)
+    wait("v", k_slq)
     done("v", v.tensor_copy(T.sla[:, 9:36], T.slq[:, 9:36]))
-    k_sl = done("v", v.tensor_copy(T.slb[:, 10:37], T.slq[:, 9:36]))
-    wait("v", k_idf)
-    k_nid = done("v", v.tensor_scalar(T.nid[:, :], T.idf[:, :], -1.0, None, MUL))
-    lists(1)
-    positions(POS[1], POS[0], T.acc)
+    k_sl = done("v", v.tensor_copy(T.slb[:, 1:37], T.slq[:, :]))
+    wait("v", k_idb)
+    for i, x in enumerate(TIMES):
+        k_times = done("v", v.tensor_scalar(T.times[:, 128 * i:128 * i + 128], T.idb[:, :], x, None, MUL))
 
     k_fac, k_stg, k_cst, k_m, k_a3 = {}, {}, {}, {}, {}
     banks = ((0, PB), (PB, M))
 
-    def factors(l, a, e):
-        wait("t", k_sel, ("ldv%d" % l, 16))
+    k_bank = {}
+
+    def block_factors(e):
+        return [k_bank[b] for b in range(e * M // PB, ((e + 1) * M - 1) // PB + 1)]
+
+    def factors(l, a, e, shift=0):
+        wait("t", k_sel if l < 3 else k_sel2, k_v[l])
+        base, p = K * ((l - 1) % 2) + shift, 32 * (l // 3)
         while a < e:
-            x = (a // PB + 1) * PB
-            k = done("t", g.tensor.matmul(T.fac[:, a:x], T.sel[0:8, :], T.vsb[0:8, K * (l - 1) + a:K * (l - 1) + x], True, True))
+            x = min(e, (a // PB + 1) * PB)
+            k = done("t", g.tensor.matmul(T.fac[:, a:x], T.sel[p:p + 8, :], T.vsb[p:p + 8, base + a:base + x], True, True))
+            k_bank[a // PB] = k
             a = x
         return k
 
@@ -314,16 +399,26 @@ def rank_program(g, core, T, topo):
         return copy(T.bsh[:, l * SH:(l + 1) * SH], T.bsb[:, l * M:(l + 1) * M].indirect(sl_cols(l, 0, 9)))
 
     k_f = {l: ("ldf%d" % l, 256) for l in range(3, 5)}
-    for l, a in ((1, 0), (2, 2 * PB)):
-        wait("t", k_sel, ("ldv%d" % l, 16))
-        for x, e in banks:
-            k = done("t", g.tensor.matmul(T.fac[:, a + x:a + e], T.sel[0:8, :], T.vsb[0:8, K * (l - 1) + x:K * (l - 1) + e], True, True))
-        wait("s", k)
-        k_f[l] = done("s", g.scalar.activation(T.valf[:, M * (l - 1):M * l], T.fac[:, a:a + M], COPY, scale=-1.0))
-    wait("t", k_f[2])
-    k_fac[1] = factors(1, NV, K)
+    wait("s", factors(1, 2 * M, K))
+    k_f[1] = done("s", g.scalar.activation(T.valf[:, vf(1, 2):vf(1, 4)], T.fac[:, 2 * M:K], COPY, scale=-1.0))
+    k_mult = multiples(CUT, M, T.acc[:, 0:M - CUT], rounded(CUT, M))
+
+    def shown_v(l):
+        wait("s", ("ldf%d" % l, 256) if l > 1 else k_f[1], k_sl)
+        return done("s", g.scalar.activation(T.vsh[:, l * SH:(l + 1) * SH], T.valf[:, vf(l, 2):vf(l, 3)].indirect(sl_cols(l, 0, 9)),
+                                             COPY, scale=-1.0))
+
+    k_vsh = shown_v(1)
+    k_round = rounded(0, CUT)
+    for l in range(1, 5):
+        lists(l)
+    wait("v", ("ldb1", 16), k_sl)
+    k_bsh = done("v", v.tensor_copy(T.bsh[:, SH:2 * SH], T.bsb[:, M:2 * M].indirect(sl_cols(1, 0, 9))))
+    positions(CUT, M, T.acc[:, 0:M - CUT], k_mult, lambda: None)
+    factors(1, 0, 2 * M)
     prep_acc(1)
-    k_bsh = shown_b(1)
+    wait("t", k_f[1])
+    k_stage = factors(2, 3 * M, K)
     scatter(0)
 
     for l in range(1, 5):
@@ -332,158 +427,240 @@ def rank_program(g, core, T, topo):
         col = 192 * (l - 1)
         k_raw = []
         wait("s", fa[l - 1], k_off[l], k_wz, k_wz2, k_y[l - 1], *([k_m[l - 1]] if l > 1 else []))
-        for a, e in CH:
-            k_raw.append(copy(T.raw[:, a - NV:e - NV], win.indirect(T.offf[:, col + a // 16:col + e // 16])))
+        for e in range(3):
+            n = PB if (l, e) == (4, 2) else M
+            a = PV if e == 1 and l < 4 else 0
+            k_raw.append(copy(T.raw[:, e * M + a:e * M + n], win.indirect(T.offf[:, col + 48 * e + a // 16:col + 48 * e + n // 16])))
         wait("v", fa[l - 1], k_off[l], k_wz, k_wz2, k_f[l], k_y[l - 1])
-        made = []
-        cs = [T.bsh[:, l * SH:(l + 1) * SH], T.c0[:, :], T.c1[:, :], T.c2[:, :], T.sh[:, l * SH:(l + 1) * SH]] if l < 4 else None
-        k_c = [k_bsh]
+        k_p = {3: done("v", v.tensor_tensor(blk[3], win.indirect(T.offf[:, col + 144:col + 192]), T.valf[:, vf(l, 3):vf(l, 4)], MUL))}
 
-        def k_p(e):
-            return min(t for t in made if t[0] >= (e + 1) * M)[1]
+        def product(e):
+            wait("v", k_raw[e], *block_factors(e))
+            n = PB if (l, e) == (4, 2) else M
+            k_p[e] = done("v", v.tensor_tensor(T.prod[:, e * M:e * M + n], T.raw[:, e * M:e * M + n], T.fac[:, e * M:e * M + n], MUL))
 
-        def shown(lag):
-            while l < 4 and len(k_c) < 5 and len(made) > lag and made[-1 - lag][0] >= len(k_c) * M:
-                e = len(k_c) - 1
-                wait("v", k_sl, k_p(e), k_c[-1])
-                k_c.append(done("v", v.tensor_tensor(cs[e + 1], blk[e].indirect(sl_cols(l, 0, 9)), cs[e], SUB if e < 2 else ADD)))
-
-        made.append((M, done("v", v.tensor_tensor(blk[0], win.indirect(T.offf[:, col:col + M // 16]), T.valf[:, M * (l - 1):M * l], MUL))))
-        for i, (a, e) in enumerate(CH):
-            wait("v", k_raw[i], k_fac[l])
-            made.append((e, done("v", v.tensor_tensor(T.prod[:, a:e], T.raw[:, a - NV:e - NV], T.fac[:, a:e], MUL))))
-            shown(1)
-        k_m[l] = made[-1][1]
-        shown(0)
-        if l < 4:
-            wait("g", k_c[-1])
-            send(l, T.sh, T.w, R, True)
+        def shown(out, window, other, op, *need):
+            wait("v", k_sl, *need)
+            return done("v", v.tensor_tensor(out, window.indirect(sl_cols(l, 0, 9)), other, op))
 
         def tensor_add(a, e, i, stop):
-            wait("t", k_p(i), k_idf, k_nid)
-            return done("t", g.tensor.matmul(T.acc[:, a:e], (T.idf if i else T.nid)[:, :], T.prod[:, i * M + a:i * M + e], False, stop))
+            wait("t", k_p[i], k_idf, k_nid)
+            return done("t", g.tensor.matmul(T.acc[:, a:e], (T.idf if i < 3 else T.nid)[:, :], T.prod[:, i * M + a:i * M + e], False, stop))
 
+        def vector_add(i, js=(0, 1)):
+            for j in js:
+                a, e = banks[j]
+                if i + 1 >= TA[l - 1][j]:
+                    wait("v", k_p[i], k_acc[j])
+                    out = T.acc[:, a:e] if i < 2 else T.w[:, l * M + a:l * M + e]
+                    k_acc[j] = done("v", v.tensor_tensor(out, T.acc[:, a:e], T.prod[:, i * M + a:i * M + e],
+                                                         SUB if (l, i, j) == (4, 2, 1) else ADD))
+
+        if PV and l < 4:
+            k_pv = done("v", v.tensor_copy(T.raw[:, M:M + PV], win.indirect(T.offf[:, col + 48:col + 48 + PV // 16])))
+        product(0)
+        if PV and l < 4:
+            wait("v", k_pv)
+        if l == 4:
+            done("v", v.tensor_tensor(T.prod[:, 2 * M + PB:3 * M], win.indirect(T.offf[:, col + 128:col + 144]),
+                                      T.valf[:, vf(4, 2) + PB:vf(4, 3)], MUL))
         k_acc = {}
-        for i in range(3):
+        for i in range(2):
             for j, (a, e) in enumerate(banks):
                 if i < TA[l - 1][j]:
-                    k_acc[j] = tensor_add(a, e, i, i == TA[l - 1][j] - 1)
-        wait("y", fa[l - 1])
-        snapshot(l - 1)
+                    k_acc[j] = tensor_add(a, e, (i + 3) % 4, i == TA[l - 1][j] - 1)
         if l < 4:
-            if l > 1:
-                ld_v("y", l + 1)
-            ld_b("y", l + 1)
+            mine = slice(l * SH, (l + 1) * SH)
+            x = shown(T.c0[:, :], blk[3], T.bsh[:, mine], SUB, k_p[3], k_bsh)
+        product(1)
+        if l < 4:
+            shown(T.sh[:, 0:SH], blk[0], T.c0[:, :], SUB, k_p[0], x, left[-1])
+            wait("v", k_p[1])
+            done("v", v.tensor_copy(T.sh[:, SH:2 * SH], blk[1].indirect(sl_cols(l, 0, 9))))
+            wait("g", shown(T.sh[:, 2 * SH:3 * SH], T.raw[:, 2 * M:3 * M], T.vsh[:, mine], MUL, k_raw[2], k_vsh))
+            send(l, T.sh, T.w, R, True)
+        snapshot(l - 1, fa[l - 1])
+        if l == 3:
+            ld_f("y", 4)
+        if l == 4:
+            vector_add(0)
+        if 2 not in k_p:
+            product(2)
+        k_m[l] = k_p[2]
+        if l < 4:
             if l < 3:
                 wait("y", left[l])
-                ld_f("y", l + 2)
-        scatter(l)
-        if l < 3:
-            k_bsh = shown_b(l + 1)
-
-        def vector_add(a, e, i, *need):
-            wait("v", k_p(i), *need)
-            out = T.acc[:, a:e] if i < 3 else T.w[:, l * M + a:l * M + e]
-            return done("v", v.tensor_tensor(out, T.acc[:, a:e], T.prod[:, i * M + a:i * M + e], ADD))
+                ld_b("y", l + 2)
+            if l == 1:
+                ld_v("y", 3)
+                ld_f("y", 3)
+            if l == 3 and EARLY:
+                wait("y", left[l])
+                ld_g("y", 4)
+                if 2 in EARLY:
+                    ld_g("y", 3)
+        if l == 4 and EARLY:
+            k_x = unknowns(3, rounded_columns(3))
+            k_vt = slot_factors(3)
+            scatter(l)
+        else:
+            scatter(l)
 
         if l == 3:
-            wait("v", ("ini", 32))
-        for i in range(1, 4):
-            for j, (a, e) in enumerate(banks):
-                if i >= TA[l - 1][j]:
-                    k_acc[j] = k_a3[l] = k_y[l] = vector_add(a, e, i, k_acc[j])
+            wait("v", ("ini", 16))
+        for i in range(3):
+            if i or l < 4:
+                vector_add(i)
+            if l == 4 and i == 1:
+                if EARLY:
+                    k_x = unknown_list(3, k_x)
+                factors(4, 5 * PB, K)
+        k_a3[l] = k_y[l] = k_acc[1]
         if l < 4:
+            if l == 2:
+                spare = T.fac[:, 5 * PB:5 * PB + CUT]
+                k_mult = multiples(0, CUT, spare, k_round)
             wait("t", k_m[l])
-            k_fac[l + 1] = factors(l + 1, NV if l < 3 else PB, K)
+            factors(l + 1, 0, (4 * PB, 3 * M, 5 * PB)[l - 1])
             prep_acc(l + 1)
-            lists(l + 1)
-            positions(POS[l + 1], POS[l], T.fac)
+            if l == 1:
+                wait("s", k_stage, k_m[1])
+                k_f[2] = done("s", g.scalar.activation(T.valf[:, vf(2, 3):vf(2, 4)], T.fac[:, 3 * M:K], COPY, scale=-1.0))
+                wait("t", k_f[2])
+                factors(2, 4 * PB, 3 * M)
+            if l < 3:
+                k_bsh = shown_b(l + 1)
+                if l + 1 in DEFER:
+                    k_vsh = shown_v(l + 1)
             if l == 3:
-                wait("t", *k_pos.values())
-                k_f4 = factors(4, 0, PB)
-            if l == 3:
-                convert(3)
-
-    SB = M - VA
+                positions(0, CUT, spare, k_mult, lambda: convert(3))
+                wait("t", k_pos[1])
 
     def start_acc(l, need):
         wait("t", need)
         bank = PB * (l % 2)
-        done("t", g.tensor.matmul(T.acc[:, bank:bank + SB], T.idf[:, :], T.w[:, l * M + VA:(l + 1) * M], True, False))
+        done("t", g.tensor.matmul(T.acc[:, bank:bank + M - VAS[l]], T.idf[:, :], T.w[:, l * M + VAS[l]:(l + 1) * M], True, False))
 
     k_z = k_a3[4]
     start_acc(3, k_z)
-    k_bf = k_f4
-    stores = 0
     for l in range(4, -1, -1):
         if l < 4:
+            VA, TB = VAS[l], TBS[l]
+            SB = M - VA
             win = T.pr[:, 0:PAD + K * (4 - l)]
             wl = T.w[:, M * l:M * (l + 1)]
             acc = T.acc[:, PB * (l % 2):PB * (l % 2) + SB]
-            wait("s", k_pr, k_list[l][1], k_pad)
-            if FOLD == 4:
+            wait("s", k_pr, k_list[l, 0], k_pad)
+            wait("v", k_pr, k_list[l, 0], k_pad)
+            if l not in EARLY:
                 wait("s", left[-1])
-                wait("g", copy(T.rsum[:, 2 * SH:4 * SH], win.indirect(T.offr[:, 36 * l:36 * l + 18])))
-            k_raw = [copy(T.raw[:, s * SB:(s + 1) * SB], win.indirect(T.offo[:, 192 * l + 48 * s + VA // 16:192 * l + 48 * (s + 1)]))
+                wait("g", copy(T.rsum[:, 0:16 * RS], win.indirect(T.offr[:, 40 * l:40 * l + RS])))
+                if RS < 36:
+                    wait("v", left[-1])
+                    wait("g", done("v", v.tensor_copy(T.rsum[:, 16 * RS:4 * SH], win.indirect(T.offr[:, 40 * l + RS:40 * l + 36]))))
+                send(l, T.rsum, T.rc, 0, False)
+            if (l, 1) not in k_list:
+                convert(l, (1,))
+            wait("s", k_list[l, 1])
+            k_raw = [copy(T.raw[:, s * SB:(s + 1) * SB] if s < 3 else T.prod[:, XA + VA:XA + M], win.indirect(T.offo[:, 192 * l + 48 * s + VA // 16:192 * l + 48 * (s + 1)]))
                      for s in range(4)]
-            wait("v", k_pr, k_list[l][0], k_pad)
-            if FOLD == 4:
-                wait("v", left[-1])
-                k_rs = done("v", v.tensor_copy(T.rsum[:, 0:2 * SH], win.indirect(T.offr[:, 36 * l + 18:36 * l + 36])))
-            else:
-                x = done("v", v.tensor_copy(T.u1[:, :], win.indirect(T.offr[:, 36 * l:36 * l + 18])))
-                wait("v", x, left[-1])
-                k_rs = done("v", v.tensor_tensor(T.rsum[:, 0:2 * SH], win.indirect(T.offr[:, 36 * l + 18:36 * l + 36]), T.u1[:, :], ADD))
-            wait("g", k_rs)
-            send(l, T.rsum, T.rc, 0, False)
-            snapshot(7 - l, *([left[-1]] if AFTER else []))
+            if l > 0 and l not in EARLY:
+                snapshot(7 - l)
+            if l == 3 and 1 in EARLY:
+                wait("y", left[-1])
+                ld_g("y", 2)
             early = set(k_snap)
-            if 8 - l < len(SLOTS):
-                scatter(8 - l)
+            if l - 1 in EARLY:
+                k_x = rounded_columns(l - 1)
             wait("t", k_pr)
             if l > 0:
-                factors(l, 0, PB)
-            for s in range(TB):
-                wait("t", k_raw[s])
-                k_t = done("t", g.tensor.matmul(acc, T.idf[:, :], T.raw[:, s * SB:(s + 1) * SB], False, s == TB - 1))
+                factors(l, 0, 2 * PB)
+            bank = PB * (l % 2)
+            for s, a, e, stop in ((0, 0, SB, False), (1, 0, SB, TB == 0), (2, 0, TB, True)):
+                if a < e:
+                    wait("t", k_raw[s])
+                    k_t = done("t", g.tensor.matmul(T.acc[:, bank + a:bank + e], T.idf[:, :], T.raw[:, s * SB + a:s * SB + e], False, stop))
+            if l - 1 in EARLY:
+                k_x = unknowns(l - 1, k_x)
             if l > 0:
-                k_bf = factors(l, PB, K)
-                start_acc(l - 1, k_z)
-            wait("v", k_list[l][1])
-            k_h = [k_z, k_z]
-            for s in range(4):
-                for h, (a, e) in enumerate(((0, VA // 2), (VA // 2, VA))):
+                factors(l, 2 * PB, 5 * PB)
+            wait("v", k_list[l, 1])
+            cut = VA // 64 * 32 if HALVES else VA
+            parts = [p for p in ((0, cut), (cut, VA)) if p[0] < p[1]]
+            k_h = [k_z for p in parts]
+
+            def own_slot(s):
+                for h, (a, e) in enumerate(parts):
                     wait("v", k_h[h])
-                    src = wl[:, a:e] if False else (T.w[:, M * l + a:M * l + e] if s == 0 else T.prod[:, M * (s - 1) + a:M * (s - 1) + e])
-                    out = T.w[:, M * l + a:M * l + e] if s == 3 else T.prod[:, M * s + a:M * s + e]
+                    at = [M * l, 0, VA, XA, M * l]
+                    src = (T.w if s == 0 else T.prod)[:, at[s] + a:at[s] + e]
+                    out = (T.w if s == 3 else T.prod)[:, at[s + 1] + a:at[s + 1] + e]
                     c = 192 * l + 48 * s
                     k_h[h] = done("v", v.tensor_tensor(out, win.indirect(T.offo[:, c + a // 16:c + e // 16]), src, ADD))
-            if l - 1 in early:
-                convert(l - 1)
-            x = k_t
-            for s in range(TB, 4):
-                wait("v", x, k_raw[s])
-                x = done("v", v.tensor_tensor(acc if s < 3 else T.w[:, M * l + VA:M * (l + 1)], acc, T.raw[:, s * SB:(s + 1) * SB], ADD))
-            wait("v", x)
-            ds = sorted(range(3), key=lambda d: topo.chip(cores[(rank + 1 + d) % N]) != topo.chip(core))
-            for d in ds:
+
+            for s in range(3):
+                own_slot(s)
+            if l > 0:
+                scatter(8 - l)
+            if l == 1:
+                snapshot(7)
+            k_acc = [k_t]
+
+            def third():
+                wait("v", k_t, k_raw[2])
+                part = T.acc[:, bank + TB:bank + SB]
+                k_acc[0] = done("v", v.tensor_tensor(part, part, T.raw[:, 2 * SB + TB:3 * SB], ADD))
+
+            fill = [lambda: convert(l - 1, (0,)), lambda: convert(l - 1, (1,))] if l - 1 in early else []
+            if TB < SB:
+                fill.append(third)
+
+            def arrival(window, d, *need):
                 a = (l * 3 + d) * S
-                wait("v", ba[l, d])
-                x = done("v", v.tensor_tensor(T.tmp[:, :], wl.indirect(sl_cols(l, d, 3)), T.rc[:, a:a + S], ADD))
-                wait("v", x)
-                k_z = done("v", v.tensor_copy(wl.indirect(sl_cols(l, d, 3)), T.tmp[:, :]))
-                wait("v", k_z)
+                wait("v", *need)
+                x = done("v", v.tensor_copy(T.tmp[:, :], window.indirect(sl_cols(l, d, 3))))
+                if fill:
+                    fill.pop(0)()
+                wait("v", x, ba[l, d])
+                x = done("v", v.tensor_tensor(window.indirect(sl_cols(l, d, 3)), T.tmp[:, :], T.rc[:, a:a + S], ADD))
+                if fill:
+                    fill.pop(0)()
+                return x
+
+            ds = sorted(range(3), key=lambda d: topo.chip(cores[(rank + 1 + d) % N]) != topo.chip(core))
+            own_slot(3)
+            if TB < SB:
+                fill.pop()()
+                if fill:
+                    fill.pop()()
+            wait("v", k_acc[0], k_raw[3])
+            k_z = done("v", v.tensor_tensor(T.w[:, M * l + VA:M * (l + 1)], acc, T.prod[:, XA + VA:XA + M], ADD))
+            if fill and FIRST:
+                fill.pop()()
+            if l > 0:
+                factors(l, 5 * PB, K)
+                start_acc(l - 1, k_h[0])
+            for d in ds[NX:]:
+                k_z = arrival(wl, d, k_z)
         zl = T.w[:, l * M:(l + 1) * M]
+        if l - 1 in EARLY:
+            wait("v", k_z, k_x, k_vt, left[-1])
+            wait("g", done("v", v.tensor_tensor(T.rsum[:, :], T.w[:, 0:R + 8].indirect(T.offx[:, 40 * l - 40:40 * l - 4]), T.vsh[:, :], MUL)))
+            send(l - 1, T.rsum, T.rc, 0, False)
+            snapshot(8 - l)
+            wait("y", left[-1])
         wait("y", k_z)
-        g.sync.dma_start(T.z[:, l * M:(l + 1) * M], zl).then_inc(T.sem["st"], 16)
-        stores += 16
+        load("y", "st", T.z[:, l * M:(l + 1) * M], zl)
         if l > 0:
-            wait("v", k_z, k_bf, k_scat[l])
+            wait("v", k_z, k_free[l])
             base = PAD + K * (4 - l)
             for e in range(4):
+                wait("v", *block_factors(e))
+                if e == 3 and (l - 1, 0) not in k_list:
+                    convert(l - 1)
                 k_pr = done("v", v.tensor_tensor(T.pr[:, base + e * M:base + (e + 1) * M], zl, T.fac[:, e * M:(e + 1) * M], MUL))
-            if l - 1 not in k_list:
-                convert(l - 1)
-    g.sync.wait_ge(T.sem["st"], stores)
+            if (l - 1, 0) not in k_list:
+                convert(l - 1, (0,))
+    wait("y", ("st", 80))
     wait("g", *left)
     wait("v", ("ss", count["ss"]), ("ts", count["ts"]), ("gs", count["gs"]))

@@ -4,34 +4,31 @@ from concourse.mybir import AluOpType, ActivationFunctionType
 LV, M, S, N = 5, 768, 48, 4
 R, SH = LV * M, (N - 1) * S
 K = 4 * M
-QN = (R + 4 * SH) // 16
 PB = 512
-EARLY = ()
-DEFER = (1, 2, 3)
-XM = 192
 PAD, LIFT = 16, 752
-NV = M
-CH = ((768, 1536), (1536, 2304), (2304, 2816), (2816, 3072))
 VAS = (512, 544, 544, 544)
-SPLIT = True
 QM, AM = 1536, 1560
-CUT = 256
-SQ = 9
 TIMES = (-64.0, 63.0, 1365 / 65536)
-TA = ((1, 1), (1, 2), (1, 2), (1, 2))
-TBS = (256, 224, 224, 224)
-HALVES = True
-XA, NX = 1152, 0
-FIRST = True
-RS = 36
-PV = 128
-B1 = True
-FOLD = 4
+TA = ((2, 1), (2, 1), (2, 1), (1, 2))
+X4 = 768
+XS = (0, 256, 256, 256)
+XA = 1152
 WIDE = 8
-SLOTS = (0, 1280, 1792, 1536, 2304, 2304, 1920, 1152)
+SLOTS = (384, 1280, 1792, 1536, 2304, 2048, 1792, 1152)
 SNAPS = {2: 3, 4: 2, 5: 1, 7: 0}
 IOTAS = SLOTS[:4] + (SLOTS[4] + SLOTS[5],) + SLOTS[6:]
-PIECE = 1024
+HALVES = ((384, 768), (0, 384))
+BL = True
+PARTS = ((576, 768), (384, 576), (0, 384))
+LOADS = (("clear",), ("b1", "f1", "f2", "b2"))
+LATE = 1
+RF = (0, 0, 0, 0)
+FB = (0, 2, 2, 2)
+CL = True
+B0 = "s"
+ZERO = 2304
+NS = 0
+TAIL = (0, 0, 0, 0)
 
 SCRATCH = {
     "w": ("sbuf", [128, R + 4 * SH], "float32"),
@@ -39,11 +36,7 @@ SCRATCH = {
     "invo": ("sbuf", [128, 768], "float32"),
     "invr": ("sbuf", [128, 4, 4, 48], "float32"),
     "pr": ("sbuf", [128, PAD + 4 * K], "float32"),
-    "valf": ("sbuf", [128, PAD + 4 * K], "bfloat16"),
-    "m768": ("sbuf", [128, 128], "bfloat16"),
-    "xt": ("sbuf", [128, 72], "bfloat16"),
-    "xn": ("sbuf", [128, 36], "float32"),
-    "offx": ("sbuf", [128, 160], "uint16"),
+    "valf": ("sbuf", [128, 4 * K], "bfloat16"),
     "vsh": ("sbuf", [128, 4 * SH], "float32"),
     "nid": ("sbuf", [128, 128], "float32"),
     "first": ("sbuf", [128, 36], "int32"),
@@ -62,12 +55,11 @@ SCRATCH = {
     "sla": ("sbuf", [128, 40], "uint16"),
     "slb": ("sbuf", [128, 40], "uint16"),
     "prod": ("sbuf", [128, K], "float32"),
-    "raw": ("sbuf", [128, K - NV], "float32"),
+    "raw": ("sbuf", [128, 2 * M + PB], "float32"),
     "bsh": ("sbuf", [128, 4 * SH], "float32"),
     "c0": ("sbuf", [128, SH], "float32"),
     "c1": ("sbuf", [128, SH], "float32"),
-    "c2": ("sbuf", [128, SH], "float32"),
-    "sh": ("sbuf", [128, 3 * SH], "float32"),
+    "sh": ("sbuf", [128, 4 * SH], "float32"),
     "rsum": ("sbuf", [128, 4 * SH], "float32"),
     "rc": ("sbuf", [128, 4 * SH], "float32"),
     "tmp": ("sbuf", [128, S], "float32"),
@@ -80,11 +72,9 @@ SCRATCH = {
     "acc": ("psum", [128, 2 * PB], "float32"),
     "fac": ("psum", [128, 6 * PB], "float32"),
 }
-SEMAPHORES = (["vs", "ss", "ts", "gs", "st", "ldsl", "ini"] + ["loc%d" % i for i in range(8)]
-              + ["snap%d" % i for i in SNAPS]
-              + ["ldb%d" % l for l in range(5)] + ["lde"]
-              + ["ldv1", "ldv3", "ldf2", "ldf3", "ldf4"] + ["ldg%d" % (h + 1) for h in EARLY] + ["fa%d" % h for h in range(4)]
-              + ["ba%d_%d" % (h, d) for h in range(4) for d in range(3)])
+SEMAPHORES = (["vs", "ss", "ts", "gs", "st", "ldsl", "ini", "lde0", "lde1", "ldv1", "ldv3"] + ["loc%d" % i for i in range(8)]
+              + ["snap%d" % i for i in SNAPS] + ["ldb%d" % l for l in range(5)] + ["ldf%d" % l for l in range(1, 5)]
+              + ["fa%d" % h for h in range(4)] + ["ba%d_%d" % (h, d) for h in range(4) for d in range(3)])
 
 
 def engine_plan(src, dsts, topo, most):
@@ -116,8 +106,8 @@ def rank_program(g, core, T, topo):
         return
     ADD, SUB, MUL = AluOpType.add, AluOpType.subtract, AluOpType.mult
     COPY, SILU = ActivationFunctionType.Copy, ActivationFunctionType.Silu
-    IDENT = COPY
     cores = list(T.cores)
+    v = g.vector
     q = {"v": g.vector, "s": g.scalar, "t": g.tensor, "g": g, "y": g.sync}
     own = {"v": "vs", "s": "ss", "t": "ts", "g": "gs"}
     count = {"vs": 0, "ss": 0, "ts": 0, "gs": 0}
@@ -139,22 +129,20 @@ def rank_program(g, core, T, topo):
         count[name] += 1
         return (name, count[name])
 
-    def copy(out, in_):
-        return done("s", g.scalar.activation(out, in_, COPY))
-
-    others = [c for c in cores if c != core]
+    def copy(out, in_, scale=1.0):
+        return done("s", g.scalar.activation(out, in_, COPY, scale=scale))
 
     def calls(r, forward):
         dsts = {cores[(r + 1 + d) % N] if forward else cores[(r - 1 - d) % N]: d for d in range(3)}
         far = [c for c in dsts if topo.chip(c) != topo.chip(cores[r])]
-        sets = [list(dsts)] if forward or not SPLIT else [[c for c in dsts if c != far[-1]], far[-1:]]
+        sets = [list(dsts)] if forward else [[c for c in dsts if c != far[-1]], far[-1:]]
         plans = [engine_plan(cores[r], x, topo, 4 if forward else WIDE) for x in sets]
         return [[(dsts[c], c, plan[c]) for c in plan] for plan in plans]
 
     arrive = {f: {cores[r]: len(e) for r in range(N) for call in calls(r, f) for d, c, e in call if c == core} for f in (True, False)}
     left = []
 
-    def send(h, src, dst, dst_base, forward):
+    def send(h, src, n, dst, dst_base, forward):
         name, local_each = "loc%d" % len(left), 0
         for call in calls(rank, forward):
             tr = []
@@ -162,7 +150,6 @@ def rank_program(g, core, T, topo):
                 rid, pid = topo.addr(c)[:2]
                 a = (h * 3 + d) * S
                 sem = T.sem["fa%d" % h] if forward else T.sem["ba%d_%d" % (h, d)]
-                n = 4 if not forward else 3 if h else 1
                 srcs = [src[:, s * SH + d * S:s * SH + (d + 1) * S] for s in range(n)]
                 tr.append(RemoteDMATransfer(dst_ids=[DstId(rid=rid, pnc=pid)], dma_engine_mask=sum(1 << e for e in engines),
                                             remote_sem=sem, srcs=srcs, dsts=[dst[:, dst_base + a:dst_base + a + S]],
@@ -190,70 +177,39 @@ def rank_program(g, core, T, topo):
                 laid.append((e, done("g", g.iota(numbers(x, e), [[1, e - x]], PAD + x + LIFT, 0,
                                                  allow_small_or_imprecise_dtypes=True))))
 
-    def rounded(a, e):
-        wait("v", ("lde", 16))
-        done("v", v.tensor_scalar(T.q16[:, a:e], T.ents[:, a:e], 1.0 / 64, QM - 0.5 + 0.5 / 64, MUL, ADD))
-        return done("v", v.tensor_scalar(T.a16[:, a:e], T.ents[:, a:e], 1.0 / K, AM - 0.5 + 0.5 / K, MUL, ADD))
-
     def multiples(a, e, psum, *need):
         wait("t", k_times, *need)
         for i, src in enumerate((T.q16, T.a16, T.q16)):
             k = done("t", g.tensor.matmul(psum, T.times[:, 128 * i:128 * i + 128], src[:, a:e], i == 0, i == 2))
         return k
 
-    def positions(a, e, psum, need, between):
+    def summed(i, need):
         wait("v", need)
-        x = done("v", v.tensor_tensor(psum, psum, T.ents[:, a:e], ADD))
-        between()
-        wait("v", x)
-        x = done("v", v.tensor_scalar(T.pos[:, a:e], psum, 64 * QM - 63 * AM - QM * TIMES[2], 48, ADD, MUL))
+        return done("v", v.tensor_tensor(spare[i], spare[i], T.ents[:, PARTS[i][0]:PARTS[i][1]], ADD))
+
+    def positions(i, need):
+        a, e = PARTS[i]
+        wait("v", need)
+        x = done("v", v.tensor_scalar(T.pos[:, a:e], spare[i], 64 * QM - 63 * AM - QM * TIMES[2], 48, ADD, MUL))
         k_pos.update({l: x for l in range(a // 192 + 1, (e - 1) // 192 + 2)})
 
-    def scatter(i, between=None):
-        a, out = sum(SLOTS[:i]), None
+    def scatter(i):
+        a = sum(SLOTS[:i])
         for x, e in pieces(a, a + SLOTS[i]):
-            if between and x > a:
-                out = between()
             l = 4 - x // K
             col = 192 * (l - 1) + (x % K) // 16
-            wait("s", ("ini", 16), k_pos[l], min(t for t in laid if t[0] >= e)[1], *last["scat"])
+            wait("s", ("ini", 32), k_pos[l], min(t for t in laid if t[0] >= e)[1], *last["scat"])
             k = done("s", g.scalar.activation(T.inv[:, :].indirect(T.pos[:, col:col + (e - x) // 16]), numbers(x, e), SILU))
             last["scat"] = [k]
             if i < 7:
                 k_free[l] = k
-        return out
-
-    def rounded_columns(h):
-        wait("s", k_snap[h])
-        src = T.invr[:, h, :, 9 * h:9 * h + 9]
-        copy(T.xn[:, :], src)
-        done("s", g.scalar.activation(T.xt[:, 0:36], src, IDENT, bias=XM - 0.5 + 0.5 / M, scale=1.0 / M))
-        return done("s", g.scalar.activation(T.xt[:, 36:72], src, IDENT, bias=XM + 0.25 + 0.5 / K, scale=1.0 / K))
-
-    def unknowns(h, need):
-        wait("t", need, k_m768)
-        for i in range(2):
-            done("t", g.tensor.matmul(T.fac[:, 5 * PB:5 * PB + 36], T.m768[:, :], T.xt[:, 36 * i:36 * i + 36], i == 0, False))
-        return done("t", g.tensor.matmul(T.fac[:, 5 * PB:5 * PB + 36], T.idf[:, :], T.xn[:, :], False, True))
-
-    def unknown_list(h, need):
-        wait("v", need)
-        k = done("v", v.tensor_scalar(T.offx[:, 40 * h:40 * h + 36], T.fac[:, 5 * PB:5 * PB + 36], R + 2 * M * XM, None, ADD))
-        wait("t", k)
-        return k
-
-    def slot_factors(h):
-        wait("s", k_list[h, 0], k_vpad, ("ldg%d" % (h + 1), 256), ("ldf%d" % (h + 1), 256))
-        return done("s", g.scalar.activation(T.vsh[:, :], T.valf[:, 0:PAD + K * (4 - h)].indirect(T.offr[:, 40 * h:40 * h + 36]),
-                                             COPY, scale=-1.0))
 
     def snapshot(i, *need):
         if i in SNAPS:
             h = SNAPS[i]
-            k = "y" if i < SQ else "s"
-            wait(k, *(last["scat"] + list(need)))
-            load(k, "snap%d" % i, T.invr[:, h, :, :], T.inv[0:128:16, 5 * K:6 * K])
-            load(k, "snap%d" % i, T.invo[:, 192 * h:192 * h + 192], T.inv[0:128:16, h * K:(h + 1) * K])
+            wait("y", *(last["scat"] + list(need)))
+            load("y", "snap%d" % i, T.invr[:, h, :, :], T.inv[0:128:16, 5 * K:6 * K])
+            load("y", "snap%d" % i, T.invo[:, 192 * h:192 * h + 192], T.inv[0:128:16, h * K:(h + 1) * K])
             k_snap[h] = ("snap%d" % i, 32)
             last["scat"] = [k_snap[h]]
 
@@ -267,40 +223,38 @@ def rank_program(g, core, T, topo):
     def load(k, name, out, in_):
         q[k].dma_start(out, in_).then_inc(T.sem[name], 16)
 
-    def ld_b(k, l):
-        load(k, "ldb%d" % l, T.bsb[:, l * M:(l + 1) * M], T.b[:, l * M:(l + 1) * M])
+    def ld_b(l):
+        load("y", "ldb%d" % l, T.bsb[:, l * M:(l + 1) * M], T.b[:, l * M:(l + 1) * M])
 
-    def ld_v(k, l):
+    def ld_v(l):
         a = K * (l - 1)
-        load(k, "ldv%d" % l, T.vsb[16 * l - 16:16 * l - 8, :], T.val[:, a:a + 2 * K])
+        load("y", "ldv%d" % l, T.vsb[16 * l - 16:16 * l - 8, :], T.val[:, a:a + 2 * K])
 
     k_v = {l: ("ldv%d" % (l - (l + 1) % 2), 16) for l in range(1, 5)}
 
-    def vf(l, e):
-        return PAD + K * (4 - l) + M * e
-
-    def spread(k, name, l, a, e):
+    def ld_f(l):
+        a = M if l < 4 else M + X4 if X4 < M else 2 * M + XS[3]
+        a, e = K * (l - 1) + a, K * (l - 1) + (2 * M if l == 1 else K)
         for c in range(16):
-            x = M - PB if l == 4 else 0
-            load(k, name, T.valf[c:128:16, vf(l, a) - x:vf(l, e)], T.val[:, K * (l - 1) + M * a - x:K * (l - 1) + M * e])
+            load("y", "ldf%d" % l, T.valf[c:128:16, a:e], T.val[:, a:e])
 
-    def ld_f(k, l):
-        spread(k, "ldf%d" % l, l, *{2: (2, 3), 3: (2 if 3 in DEFER else 3, 4), 4: (3, 4)}[l])
+    def valf(l, a, e):
+        return T.valf[:, K * (l - 1) + a:K * (l - 1) + e]
 
-    def ld_g(k, l):
-        spread(k, "ldg%d" % l, l, 0, 3 if l == 4 else 2)
+    def clear():
+        wait("y", k_wz)
+        load("y", "ini", T.inv[0:128:16, 0:4 * K], T.w[:, ZERO:ZERO + 4 * K // 16])
+        load("y", "ini", T.inv[0:128:16, 5 * K:6 * K], T.w[:, ZERO:ZERO + K // 16])
 
     load("s", "ldsl", T.slr[:, :], T.sl[:, :])
-    ld_b("y", 0)
-    wait("y", ("ldsl", 16))
-    load("y", "lde", T.ents[:, :], T.ent[:, :])
-    k_ent = {l: ("lde", 16) for l in range(1, 5)}
+    ld_b(0)
+    ld_v(1)
+    for i, (a, e) in enumerate(HALVES):
+        load("y", "lde%d" % i, T.ents[:, a:e], T.ent[:, a:e])
 
-    v = g.vector
     k_neg = done("v", v.memset(T.negb[:, :], -1.0))
     k_oneb = done("v", v.memset(T.oneb[:, :], 1.0))
-    k_wz = done("v", v.memset(T.w[:, 2304:3840], 0.0))
-    k_pad = done("v", v.memset(T.pr[:, 0:PAD], 0.0))
+    k_wz = done("v", v.memset(T.w[:, ZERO:ZERO + M], 0.0))
     k_first = done("g", g.iota(T.first[:, :], [[M, 4], [0, 9]], 0, 0))
     wait("g", k_neg)
 
@@ -311,19 +265,11 @@ def rank_program(g, core, T, topo):
     k_sel = selection(0)
     wait("g", k_oneb)
     k_idb = done("g", g.affine_select(T.idb[:, :], T.oneb[:, :], [[-1, 128]], AluOpType.is_equal, 0.0, 0, 1))
-    lay(0)
     wait("s", k_wz)
-    k_wz2 = done("s", g.scalar.activation(T.w[:, 768:2304], T.w[:, 2304:3840], SILU))
-    ld_v("y", 1)
-    if B1:
-        ld_b("y", 1)
-
-    def clear():
-        wait("y", k_wz)
-        load("y", "ini", T.inv[0:128:16, :], T.w[:, 2304:2304 + 6 * K // 16])
-
-    if SLOTS[0]:
-        clear()
+    k_pad = done("s", g.scalar.activation(T.pr[:, 0:PAD], T.w[:, ZERO:ZERO + PAD], SILU))
+    start = {"clear": clear, "b1": lambda: ld_b(1), "f1": lambda: ld_f(1), "b2": lambda: ld_b(2), "f2": lambda: ld_f(2)}
+    for name in LOADS[0]:
+        start[name]()
 
     wait("v", ("ldsl", 16))
     k_sl = done("v", v.tensor_copy(T.sla[:, 0:9], T.slr[:, 0:9]))
@@ -337,32 +283,24 @@ def rank_program(g, core, T, topo):
     wait("v", ("ldb0", 16), k_sl)
     k_sh = done("v", v.tensor_copy(T.sh[:, 0:SH], T.bsb[:, 0:M].indirect(sl_cols(0, 0, 9))))
     wait("g", k_sh)
-    send(0, T.sh, T.w, R, True)
-    wait("g", k_wz, k_oneb)
-    k_idf = done("g", g.affine_select(T.idf[:, :], T.w[:, 3584:3712], [[-1, 128]], AluOpType.not_equal, 1.0, 0, 1))
-    k_nid = done("g", g.affine_select(T.nid[:, :], T.w[:, 3584:3712], [[-1, 128]], AluOpType.not_equal, -1.0, 0, 1))
+    send(0, T.sh, 1, T.w, R, True)
+    lay(0)
     lay(1)
-    wait("g", laid[-1][1])
+    wait("g", k_wz)
+    k_nid = done("g", g.affine_select(T.nid[:, :], T.w[:, ZERO:ZERO + 128], [[-1, 128]], AluOpType.not_equal, -1.0, 0, 1))
+    k_idf = done("g", g.affine_select(T.idf[:, :], T.w[:, ZERO:ZERO + 128], [[-1, 128]], AluOpType.not_equal, 1.0, 0, 1))
+    wait("g", k_idf)
     k_sel2 = selection(32)
     wait("g", k_sel2)
     wait("y", left[0])
-    if not B1:
-        ld_b("y", 1)
-    if not SLOTS[0]:
-        clear()
-    ld_b("y", 2)
-    if 2 in DEFER:
-        ld_f("y", 2)
+    for name in LOADS[1]:
+        start[name]()
 
-    wait("s", ("ldb0", 16))
-    k_y = {0: copy(T.w[:, 0:M], T.bsb[:, 0:M])}
-
-    k_off = {}
-
-    def lists(l):
-        a = 192 * (l - 1)
-        wait("v", k_ent[l])
-        k_off[l] = done("v", v.tensor_scalar(T.offf[:, a:a + 192], T.ents[:, a:a + 192], 0.25, -0.375, MUL, ADD))
+    if B0 == "s":
+        wait("s", ("ldb0", 16))
+        k_y = {0: copy(T.w[:, 0:M], T.bsb[:, 0:M])}
+    else:
+        k_y = {0: done("v", v.tensor_copy(T.w[:, 0:M], T.bsb[:, 0:M]))}
 
     wait("v", k_slq)
     done("v", v.tensor_copy(T.sla[:, 9:36], T.slq[:, 9:36]))
@@ -371,17 +309,15 @@ def rank_program(g, core, T, topo):
     for i, x in enumerate(TIMES):
         k_times = done("v", v.tensor_scalar(T.times[:, 128 * i:128 * i + 128], T.idb[:, :], x, None, MUL))
 
-    k_fac, k_stg, k_cst, k_m, k_a3 = {}, {}, {}, {}, {}
     banks = ((0, PB), (PB, M))
+    k_bank, k_m = {}, {}
 
-    k_bank = {}
+    def block_factors(e, n=M):
+        return [k_bank[b] for b in range(e * M // PB, (e * M + n - 1) // PB + 1)]
 
-    def block_factors(e):
-        return [k_bank[b] for b in range(e * M // PB, ((e + 1) * M - 1) // PB + 1)]
-
-    def factors(l, a, e, shift=0):
+    def factors(l, a, e):
         wait("t", k_sel if l < 3 else k_sel2, k_v[l])
-        base, p = K * ((l - 1) % 2) + shift, 32 * (l // 3)
+        base, p = K * ((l - 1) % 2), 32 * (l // 3)
         while a < e:
             x = min(e, (a // PB + 1) * PB)
             k = done("t", g.tensor.matmul(T.fac[:, a:x], T.sel[p:p + 8, :], T.vsb[p:p + 8, base + a:base + x], True, True))
@@ -389,205 +325,226 @@ def rank_program(g, core, T, topo):
             a = x
         return k
 
-    def prep_acc(l):
-        wait("t", k_idb, ("ldb%d" % l, 16), *([k_a3[l - 1]] if l > 1 else k_pos.values()))
-        for a, e in banks:
-            done("t", g.tensor.matmul(T.acc[:, a:e], T.idb[:, :], T.bsb[:, l * M + a:l * M + e], True, False))
-
     def shown_b(l):
         wait("s", ("ldb%d" % l, 16), k_sl)
         return copy(T.bsh[:, l * SH:(l + 1) * SH], T.bsb[:, l * M:(l + 1) * M].indirect(sl_cols(l, 0, 9)))
 
-    k_f = {l: ("ldf%d" % l, 256) for l in range(3, 5)}
-    wait("s", factors(1, 2 * M, K))
-    k_f[1] = done("s", g.scalar.activation(T.valf[:, vf(1, 2):vf(1, 4)], T.fac[:, 2 * M:K], COPY, scale=-1.0))
-    k_mult = multiples(CUT, M, T.acc[:, 0:M - CUT], rounded(CUT, M))
-
     def shown_v(l):
-        wait("s", ("ldf%d" % l, 256) if l > 1 else k_f[1], k_sl)
-        return done("s", g.scalar.activation(T.vsh[:, l * SH:(l + 1) * SH], T.valf[:, vf(l, 2):vf(l, 3)].indirect(sl_cols(l, 0, 9)),
-                                             COPY, scale=-1.0))
+        wait("s", ("ldf%d" % l, 256), k_sl)
+        return copy(T.vsh[:, l * SH:(l + 1) * SH], valf(l, M, 2 * M).indirect(sl_cols(l, 0, 9)), -1.0)
 
-    k_vsh = shown_v(1)
-    k_round = rounded(0, CUT)
-    for l in range(1, 5):
-        lists(l)
-    wait("v", ("ldb1", 16), k_sl)
-    k_bsh = done("v", v.tensor_copy(T.bsh[:, SH:2 * SH], T.bsb[:, M:2 * M].indirect(sl_cols(1, 0, 9))))
-    positions(CUT, M, T.acc[:, 0:M - CUT], k_mult, lambda: None)
+    k_f = {(l, e): ("ldf%d" % l, 256) for l in range(2, 5) for e in (1, 2, 3)}
+    factors(1, 4 * PB, K)
+    wait("s", k_bank[5])
+    k_f[1, 3] = copy(valf(1, 4 * PB, K), T.fac[:, 4 * PB:K], -1.0)
+    wait("s", factors(1, 3 * PB, 4 * PB))
+    k_f[1, 2] = copy(valf(1, 3 * PB + XS[0], 4 * PB), T.fac[:, 3 * PB + XS[0]:4 * PB], -1.0)
+    spare = [x[:, a:a + e - b] for (x, a), (b, e) in zip(((T.acc, 0), (T.acc, PB), (T.fac, 5 * PB)), PARTS)]
+
+    def sixty_fourths(i):
+        a, e = HALVES[i]
+        wait("v", ("lde%d" % i, 16))
+        return done("v", v.tensor_scalar(T.q16[:, a:e], T.ents[:, a:e], 1.0 / 64, QM - 0.5 + 0.5 / 64, MUL, ADD))
+
+    def areas(i, need):
+        a, e = HALVES[i]
+        wait("v", need)
+        return done("v", v.tensor_scalar(T.a16[:, a:e], T.q16[:, a:e], 1.0 / 48, AM - QM // 48 - 0.5 + 0.5 / 48, MUL, ADD))
+
+    def places(i):
+        a, e = HALVES[i]
+        return done("v", v.tensor_scalar(T.offf[:, a:e], T.ents[:, a:e], 0.25, -0.375, MUL, ADD))
+
+    x = areas(0, sixty_fourths(0))
+    k_mult = [multiples(*PARTS[i], spare[i], x) for i in range(2)]
     factors(1, 0, 2 * M)
-    prep_acc(1)
-    wait("t", k_f[1])
-    k_stage = factors(2, 3 * M, K)
+    places(0)
+    x = sixty_fourths(1)
+    y = summed(0, k_mult[0])
+    k_round = areas(1, x)
+    positions(0, y)
+    y = summed(1, k_mult[1])
+    k_off = places(1)
+    positions(1, y)
     scatter(0)
+    picks = []
 
+    order = (3, 2, 0, 1)
     for l in range(1, 5):
         win = T.w[:, 0:R + SH * l]
         blk = [T.prod[:, e * M:(e + 1) * M] for e in range(4)]
         col = 192 * (l - 1)
-        k_raw = []
-        wait("s", fa[l - 1], k_off[l], k_wz, k_wz2, k_y[l - 1], *([k_m[l - 1]] if l > 1 else []))
-        for e in range(3):
-            n = PB if (l, e) == (4, 2) else M
-            a = PV if e == 1 and l < 4 else 0
-            k_raw.append(copy(T.raw[:, e * M + a:e * M + n], win.indirect(T.offf[:, col + 48 * e + a // 16:col + 48 * e + n // 16])))
-        wait("v", fa[l - 1], k_off[l], k_wz, k_wz2, k_f[l], k_y[l - 1])
-        k_p = {3: done("v", v.tensor_tensor(blk[3], win.indirect(T.offf[:, col + 144:col + 192]), T.valf[:, vf(l, 3):vf(l, 4)], MUL))}
+        n1 = X4 if l == 4 else M
+        wait("s", fa[l - 1], k_off, k_y[l - 1], *([k_m[l - 1]] if l > 1 else []))
+        k_raw = {}
+        n2 = XS[l - 1]
+        for e, n in ((2, n2), (0, M), (1, n1)):
+            if n:
+                k_raw[e] = copy(T.raw[:, e * M:e * M + n], win.indirect(T.offf[:, col + 48 * e:col + 48 * e + n // 16]), -1.0 if e == 2 else 1.0)
+            if (l, e) == (1, 1 if BL else 0):
+                k_bsh = shown_b(1)
+        if l == 1:
+            k_vsh = shown_v(1)
+        wait("v", fa[l - 1], k_off, k_y[l - 1], *picks)
+        k_p, k_acc = {}, {}
+        b_last = BL and l == 1
 
-        def product(e):
-            wait("v", k_raw[e], *block_factors(e))
-            n = PB if (l, e) == (4, 2) else M
+        def fused(e, a):
+            wait("v", k_f[l, e])
+            return done("v", v.tensor_tensor(T.prod[:, e * M + a:(e + 1) * M], win.indirect(T.offf[:, col + 48 * e + a // 16:col + 48 * e + 48]),
+                                             valf(l, e * M + a, (e + 1) * M), MUL))
+
+        def product(e, n):
+            wait("v", k_raw[e], *block_factors(e, n))
             k_p[e] = done("v", v.tensor_tensor(T.prod[:, e * M:e * M + n], T.raw[:, e * M:e * M + n], T.fac[:, e * M:e * M + n], MUL))
 
         def shown(out, window, other, op, *need):
             wait("v", k_sl, *need)
             return done("v", v.tensor_tensor(out, window.indirect(sl_cols(l, 0, 9)), other, op))
 
-        def tensor_add(a, e, i, stop):
-            wait("t", k_p[i], k_idf, k_nid)
-            return done("t", g.tensor.matmul(T.acc[:, a:e], (T.idf if i < 3 else T.nid)[:, :], T.prod[:, i * M + a:i * M + e], False, stop))
+        def tensor_add(j, i):
+            a, e = banks[j]
+            wait("t", k_two if (i, j) == (1, 1) else k_p[order[i]], k_nid)
+            k_acc[j] = done("t", g.tensor.matmul(T.acc[:, a:e], T.nid[:, :], T.prod[:, order[i] * M + a:order[i] * M + e],
+                                                 b_last and i == 0, not b_last and i == TA[l - 1][j] - 1))
 
-        def vector_add(i, js=(0, 1)):
-            for j in js:
+        def vector_add(i):
+            for j in sorted(range(2), key=lambda j: TA[l - 1][j]):
                 a, e = banks[j]
-                if i + 1 >= TA[l - 1][j]:
-                    wait("v", k_p[i], k_acc[j])
-                    out = T.acc[:, a:e] if i < 2 else T.w[:, l * M + a:l * M + e]
-                    k_acc[j] = done("v", v.tensor_tensor(out, T.acc[:, a:e], T.prod[:, i * M + a:i * M + e],
-                                                         SUB if (l, i, j) == (4, 2, 1) else ADD))
+                if i >= TA[l - 1][j]:
+                    wait("v", k_p[order[i]], k_acc[j])
+                    out = T.acc[:, a:e] if i < 3 else T.w[:, l * M + a:l * M + e]
+                    k_y[l] = k_acc[j] = done("v", v.tensor_tensor(out, T.acc[:, a:e], T.prod[:, order[i] * M + a:order[i] * M + e],
+                                                                  SUB if i < 2 or (i == 3 and a >= n1) else ADD))
 
-        if PV and l < 4:
-            k_pv = done("v", v.tensor_copy(T.raw[:, M:M + PV], win.indirect(T.offf[:, col + 48:col + 48 + PV // 16])))
-        product(0)
-        if PV and l < 4:
-            wait("v", k_pv)
-        if l == 4:
-            done("v", v.tensor_tensor(T.prod[:, 2 * M + PB:3 * M], win.indirect(T.offf[:, col + 128:col + 144]),
-                                      T.valf[:, vf(4, 2) + PB:vf(4, 3)], MUL))
-        k_acc = {}
+        k_p[3] = fused(3, 0)
+        k_p[2] = k_two = fused(2, n2)
+        if n2:
+            product(2, n2)
+        wait("t", k_y[l - 1], k_idb, *k_pos.values())
+
+        def with_b(j, first):
+            a, e = banks[j]
+            wait("t", ("ldb%d" % l, 16))
+            k_acc[j] = done("t", g.tensor.matmul(T.acc[:, a:e], T.idb[:, :], T.bsb[:, l * M + a:l * M + e], first, not first))
+
+        if not b_last:
+            with_b(0, True)
+            with_b(1, True)
         for i in range(2):
-            for j, (a, e) in enumerate(banks):
+            for j in sorted(range(2), key=lambda j: TA[l - 1][j]):
                 if i < TA[l - 1][j]:
-                    k_acc[j] = tensor_add(a, e, (i + 3) % 4, i == TA[l - 1][j] - 1)
+                    tensor_add(j, i)
+                    if b_last and i == TA[l - 1][j] - 1:
+                        with_b(j, False)
         if l < 4:
             mine = slice(l * SH, (l + 1) * SH)
-            x = shown(T.c0[:, :], blk[3], T.bsh[:, mine], SUB, k_p[3], k_bsh)
-        product(1)
-        if l < 4:
-            shown(T.sh[:, 0:SH], blk[0], T.c0[:, :], SUB, k_p[0], x, left[-1])
-            wait("v", k_p[1])
-            done("v", v.tensor_copy(T.sh[:, SH:2 * SH], blk[1].indirect(sl_cols(l, 0, 9))))
-            wait("g", shown(T.sh[:, 2 * SH:3 * SH], T.raw[:, 2 * M:3 * M], T.vsh[:, mine], MUL, k_raw[2], k_vsh))
-            send(l, T.sh, T.w, R, True)
-        snapshot(l - 1, fa[l - 1])
-        if l == 3:
-            ld_f("y", 4)
-        if l == 4:
-            vector_add(0)
-        if 2 not in k_p:
-            product(2)
-        k_m[l] = k_p[2]
-        if l < 4:
-            if l < 3:
-                wait("y", left[l])
-                ld_b("y", l + 2)
-            if l == 1:
-                ld_v("y", 3)
-                ld_f("y", 3)
-            if l == 3 and EARLY:
-                wait("y", left[l])
-                ld_g("y", 4)
-                if 2 in EARLY:
-                    ld_g("y", 3)
-        if l == 4 and EARLY:
-            k_x = unknowns(3, rounded_columns(3))
-            k_vt = slot_factors(3)
-            scatter(l)
+            picks = []
+            for i in range(NS):
+                wait("s", k_p[3 - i], left[-1])
+                picks.append(copy(T.sh[:, (2 + i) * SH:(3 + i) * SH], blk[3 - i].indirect(sl_cols(l, 0, 9)), -1.0))
+            x, part = k_bsh, T.bsh[:, mine]
+            if b_last:
+                product(0, M)
+            if NS == 0:
+                x, part = shown(T.c0[:, :], blk[3], part, SUB, k_p[3], x), T.c0[:, :]
+            if not b_last:
+                product(0, M)
+            if NS < 2:
+                x, part = shown(T.c1[:, :], blk[2], part, SUB if NS else ADD, k_p[2], x), T.c1[:, :]
+            shown(T.sh[:, SH:2 * SH], T.raw[:, M:2 * M], T.vsh[:, mine], MUL, k_raw[1], k_vsh, left[-1])
+            wait("g", shown(T.sh[:, 0:SH], blk[0], part, SUB if NS < 2 else ADD, k_p[0], x), *picks)
+            send(l, T.sh, 2 + NS, T.w, R, True)
         else:
-            scatter(l)
-
-        if l == 3:
-            wait("v", ("ini", 16))
-        for i in range(3):
-            if i or l < 4:
-                vector_add(i)
-            if l == 4 and i == 1:
-                if EARLY:
-                    k_x = unknown_list(3, k_x)
-                factors(4, 5 * PB, K)
-        k_a3[l] = k_y[l] = k_acc[1]
+            factors(4, 4 * PB if n2 else 3 * PB, K)
+            if n1 < M:
+                fused(1, n1)
+            product(0, M)
+        snapshot(l - 1, fa[l - 1])
+        vector_add(1)
+        product(1, n1)
+        k_m[l] = k_p[1]
         if l < 4:
-            if l == 2:
-                spare = T.fac[:, 5 * PB:5 * PB + CUT]
-                k_mult = multiples(0, CUT, spare, k_round)
-            wait("t", k_m[l])
-            factors(l + 1, 0, (4 * PB, 3 * M, 5 * PB)[l - 1])
-            prep_acc(l + 1)
+            wait("y", left[l])
             if l == 1:
-                wait("s", k_stage, k_m[1])
-                k_f[2] = done("s", g.scalar.activation(T.valf[:, vf(2, 3):vf(2, 4)], T.fac[:, 3 * M:K], COPY, scale=-1.0))
-                wait("t", k_f[2])
-                factors(2, 4 * PB, 3 * M)
+                ld_v(3)
             if l < 3:
-                k_bsh = shown_b(l + 1)
-                if l + 1 in DEFER:
-                    k_vsh = shown_v(l + 1)
+                ld_b(l + 2)
+                ld_f(l + 2)
+        scatter(l)
+        if l == 3:
+            wait("v", ("ini", 32))
+        vector_add(2)
+        if l == LATE + 1:
+            k_sum = summed(2, k_mult)
+        vector_add(3)
+        if l == LATE + 1:
+            positions(2, k_sum)
+        if l < 4:
+            wait("t", k_f[1, 2])
+            if l == LATE:
+                k_mult = multiples(*PARTS[2], spare[2], k_round)
+            wait("t", k_m[l])
+            if XS[l]:
+                factors(l + 1, 2 * M, 4 * PB if l == 3 else 2 * M + XS[l])
+            factors(l + 1, 0, 2 * M)
+            if l < 3:
+                k_bsh, k_vsh = shown_b(l + 1), shown_v(l + 1)
             if l == 3:
-                positions(0, CUT, spare, k_mult, lambda: convert(3))
-                wait("t", k_pos[1])
+                convert(3)
 
     def start_acc(l, need):
-        wait("t", need)
+        wait("t", need, k_idf)
         bank = PB * (l % 2)
         done("t", g.tensor.matmul(T.acc[:, bank:bank + M - VAS[l]], T.idf[:, :], T.w[:, l * M + VAS[l]:(l + 1) * M], True, False))
 
-    k_z = k_a3[4]
+    k_z = k_y[4]
     start_acc(3, k_z)
     for l in range(4, -1, -1):
         if l < 4:
-            VA, TB = VAS[l], TBS[l]
+            VA = VAS[l]
             SB = M - VA
             win = T.pr[:, 0:PAD + K * (4 - l)]
             wl = T.w[:, M * l:M * (l + 1)]
             acc = T.acc[:, PB * (l % 2):PB * (l % 2) + SB]
-            wait("s", k_pr, k_list[l, 0], k_pad)
+            wait("s", k_pr, k_list[l, 0], k_pad, left[-1])
             wait("v", k_pr, k_list[l, 0], k_pad)
-            if l not in EARLY:
-                wait("s", left[-1])
-                wait("g", copy(T.rsum[:, 0:16 * RS], win.indirect(T.offr[:, 40 * l:40 * l + RS])))
-                if RS < 36:
-                    wait("v", left[-1])
-                    wait("g", done("v", v.tensor_copy(T.rsum[:, 16 * RS:4 * SH], win.indirect(T.offr[:, 40 * l + RS:40 * l + 36]))))
-                send(l, T.rsum, T.rc, 0, False)
-            if (l, 1) not in k_list:
-                convert(l, (1,))
-            wait("s", k_list[l, 1])
-            k_raw = [copy(T.raw[:, s * SB:(s + 1) * SB] if s < 3 else T.prod[:, XA + VA:XA + M], win.indirect(T.offo[:, 192 * l + 48 * s + VA // 16:192 * l + 48 * (s + 1)]))
-                     for s in range(4)]
-            if l > 0 and l not in EARLY:
+
+            def raw_slot(s):
+                wait("s", k_list[l, 1])
+                return copy(T.raw[:, s * SB:(s + 1) * SB] if s < 3 else T.prod[:, XA + VA:XA + M],
+                            win.indirect(T.offo[:, 192 * l + 48 * s + VA // 16:192 * l + 48 * (s + 1)]))
+
+            k_raw = [raw_slot(s) for s in range(RF[l])]
+            if TAIL[l] == 0:
+                wait("g", copy(T.rsum[:, :], win.indirect(T.offr[:, 40 * l:40 * l + 36])))
+                send(l, T.rsum, 4, T.rc, 0, False)
+            else:
+                lo, hi = (win.indirect(T.offr[:, 40 * l + c:40 * l + c + 18]) for c in (0, 18))
+                wait("v", left[-1])
+                if TAIL[l] == 3:
+                    wait("g", copy(T.rsum[:, 0:2 * SH], lo), done("v", v.tensor_copy(T.rsum[:, 2 * SH:4 * SH], hi)))
+                    send(l, T.rsum, 4, T.rc, 0, False)
+                else:
+                    wait("v", done("v", v.tensor_copy(T.rsum[:, 2 * SH:4 * SH], lo)) if TAIL[l] == 1 else copy(T.rsum[:, 2 * SH:4 * SH], lo))
+                    wait("g", done("v", v.tensor_tensor(T.rsum[:, 0:2 * SH], hi, T.rsum[:, 2 * SH:4 * SH], ADD)))
+                    send(l, T.rsum, 2, T.rc, 0, False)
+            k_raw += [raw_slot(s) for s in range(RF[l], 4)]
+            if l > 0:
                 snapshot(7 - l)
-            if l == 3 and 1 in EARLY:
-                wait("y", left[-1])
-                ld_g("y", 2)
             early = set(k_snap)
-            if l - 1 in EARLY:
-                k_x = rounded_columns(l - 1)
             wait("t", k_pr)
             if l > 0:
-                factors(l, 0, 2 * PB)
-            bank = PB * (l % 2)
-            for s, a, e, stop in ((0, 0, SB, False), (1, 0, SB, TB == 0), (2, 0, TB, True)):
-                if a < e:
-                    wait("t", k_raw[s])
-                    k_t = done("t", g.tensor.matmul(T.acc[:, bank + a:bank + e], T.idf[:, :], T.raw[:, s * SB + a:s * SB + e], False, stop))
-            if l - 1 in EARLY:
-                k_x = unknowns(l - 1, k_x)
+                factors(l, 0, FB[l] * PB)
+            for s in range(3):
+                wait("t", k_raw[s])
+                k_t = done("t", g.tensor.matmul(acc, T.idf[:, :], T.raw[:, s * SB:(s + 1) * SB], False, s == 2))
             if l > 0:
-                factors(l, 2 * PB, 5 * PB)
+                factors(l, FB[l] * PB, 5 * PB)
             wait("v", k_list[l, 1])
-            cut = VA // 64 * 32 if HALVES else VA
-            parts = [p for p in ((0, cut), (cut, VA)) if p[0] < p[1]]
-            k_h = [k_z for p in parts]
+            cut = VA // 64 * 32
+            parts = ((0, cut), (cut, VA))
+            k_h = [k_z, k_z]
 
             def own_slot(s):
                 for h, (a, e) in enumerate(parts):
@@ -604,51 +561,29 @@ def rank_program(g, core, T, topo):
                 scatter(8 - l)
             if l == 1:
                 snapshot(7)
-            k_acc = [k_t]
-
-            def third():
-                wait("v", k_t, k_raw[2])
-                part = T.acc[:, bank + TB:bank + SB]
-                k_acc[0] = done("v", v.tensor_tensor(part, part, T.raw[:, 2 * SB + TB:3 * SB], ADD))
-
             fill = [lambda: convert(l - 1, (0,)), lambda: convert(l - 1, (1,))] if l - 1 in early else []
-            if TB < SB:
-                fill.append(third)
 
-            def arrival(window, d, *need):
+            def arrival(d, *need):
                 a = (l * 3 + d) * S
                 wait("v", *need)
-                x = done("v", v.tensor_copy(T.tmp[:, :], window.indirect(sl_cols(l, d, 3))))
+                x = done("v", v.tensor_copy(T.tmp[:, :], wl.indirect(sl_cols(l, d, 3))))
                 if fill:
                     fill.pop(0)()
                 wait("v", x, ba[l, d])
-                x = done("v", v.tensor_tensor(window.indirect(sl_cols(l, d, 3)), T.tmp[:, :], T.rc[:, a:a + S], ADD))
-                if fill:
-                    fill.pop(0)()
-                return x
+                return done("v", v.tensor_tensor(wl.indirect(sl_cols(l, d, 3)), T.tmp[:, :], T.rc[:, a:a + S], ADD))
 
             ds = sorted(range(3), key=lambda d: topo.chip(cores[(rank + 1 + d) % N]) != topo.chip(core))
             own_slot(3)
-            if TB < SB:
-                fill.pop()()
-                if fill:
-                    fill.pop()()
-            wait("v", k_acc[0], k_raw[3])
+            wait("v", k_t, k_raw[3])
             k_z = done("v", v.tensor_tensor(T.w[:, M * l + VA:M * (l + 1)], acc, T.prod[:, XA + VA:XA + M], ADD))
-            if fill and FIRST:
+            if fill:
                 fill.pop()()
             if l > 0:
                 factors(l, 5 * PB, K)
                 start_acc(l - 1, k_h[0])
-            for d in ds[NX:]:
-                k_z = arrival(wl, d, k_z)
+            for d in ds:
+                k_z = arrival(d, k_z)
         zl = T.w[:, l * M:(l + 1) * M]
-        if l - 1 in EARLY:
-            wait("v", k_z, k_x, k_vt, left[-1])
-            wait("g", done("v", v.tensor_tensor(T.rsum[:, :], T.w[:, 0:R + 8].indirect(T.offx[:, 40 * l - 40:40 * l - 4]), T.vsh[:, :], MUL)))
-            send(l - 1, T.rsum, T.rc, 0, False)
-            snapshot(8 - l)
-            wait("y", left[-1])
         wait("y", k_z)
         load("y", "st", T.z[:, l * M:(l + 1) * M], zl)
         if l > 0:
@@ -656,11 +591,11 @@ def rank_program(g, core, T, topo):
             base = PAD + K * (4 - l)
             for e in range(4):
                 wait("v", *block_factors(e))
-                if e == 3 and (l - 1, 0) not in k_list:
+                if e == 3 and (l - 1, 0) not in k_list and not CL:
                     convert(l - 1)
                 k_pr = done("v", v.tensor_tensor(T.pr[:, base + e * M:base + (e + 1) * M], zl, T.fac[:, e * M:(e + 1) * M], MUL))
             if (l - 1, 0) not in k_list:
-                convert(l - 1, (0,))
+                convert(l - 1)
     wait("y", ("st", 80))
     wait("g", *left)
     wait("v", ("ss", count["ss"]), ("ts", count["ts"]), ("gs", count["gs"]))

from concourse.bass import DstId, RemoteDMATransfer
from concourse.mybir import AluOpType, ActivationFunctionType

LV, M, S, N = 5, 768, 48, 4
R, SH = LV * M, (N - 1) * S
K = 4 * M
PB = 512
PAD, LIFT = 16, 752
VAS = (512, 544, 544, 544)
QM, AM = 1536, 1560
TIMES = (-64.0, 63.0, 1365 / 65536)
TA = ((2, 1), (2, 1), (2, 1), (1, 2))
X4 = 768
XS = (0, 256, 256, 256)
XA = 1152
WIDE = 8
SLOTS = (384, 1280, 1792, 1536, 2304, 2048, 1792, 1152)
SNAPS = {2: 3, 4: 2, 5: 1, 7: 0}
IOTAS = SLOTS[:4] + (SLOTS[4] + SLOTS[5],) + SLOTS[6:]
HALVES = ((384, 768), (0, 384))
BL = True
PARTS = ((576, 768), (384, 576), (0, 384))
LOADS = (("clear",), ("b1", "f1", "f2", "b2"))
LATE = 1
RF = (0, 0, 0, 0)
FB = (0, 2, 2, 2)
CL = True
B0 = "s"
ZERO = 2304
NS = 0
TAIL = (0, 0, 0, 0)

SCRATCH = {
    "w": ("sbuf", [128, R + 4 * SH], "float32"),
    "inv": ("sbuf", [128, 6 * K], "float32"),
    "invo": ("sbuf", [128, 768], "float32"),
    "invr": ("sbuf", [128, 4, 4, 48], "float32"),
    "pr": ("sbuf", [128, PAD + 4 * K], "float32"),
    "valf": ("sbuf", [128, 4 * K], "bfloat16"),
    "vsh": ("sbuf", [128, 4 * SH], "float32"),
    "nid": ("sbuf", [128, 128], "float32"),
    "first": ("sbuf", [128, 36], "int32"),
    "bsb": ("sbuf", [128, R], "bfloat16"),
    "vsb": ("sbuf", [128, 2 * K], "bfloat16"),
    "ents": ("sbuf", [128, 768], "int32"),
    "q16": ("sbuf", [128, 768], "float16"),
    "a16": ("sbuf", [128, 768], "float16"),
    "times": ("sbuf", [128, 384], "float16"),
    "offf": ("sbuf", [128, 768], "uint16"),
    "pos": ("sbuf", [128, 768], "uint16"),
    "offo": ("sbuf", [128, 768], "uint16"),
    "offr": ("sbuf", [128, 160], "uint16"),
    "slr": ("sbuf", [128, 36], "int32"),
    "slq": ("sbuf", [128, 36], "int32"),
    "sla": ("sbuf", [128, 40], "uint16"),
    "slb": ("sbuf", [128, 40], "uint16"),
    "prod": ("sbuf", [128, K], "float32"),
    "raw": ("sbuf", [128, 2 * M + PB], "float32"),
    "bsh": ("sbuf", [128, 4 * SH], "float32"),
    "c0": ("sbuf", [128, SH], "float32"),
    "c1": ("sbuf", [128, SH], "float32"),
    "sh": ("sbuf", [128, 4 * SH], "float32"),
    "rsum": ("sbuf", [128, 4 * SH], "float32"),
    "rc": ("sbuf", [128, 4 * SH], "float32"),
    "tmp": ("sbuf", [128, S], "float32"),
    "negb": ("sbuf", [128, 128], "bfloat16"),
    "sel0": ("sbuf", [128, 128], "bfloat16"),
    "sel": ("sbuf", [128, 128], "bfloat16"),
    "oneb": ("sbuf", [128, 128], "bfloat16"),
    "idb": ("sbuf", [128, 128], "bfloat16"),
    "idf": ("sbuf", [128, 128], "float32"),
    "acc": ("psum", [128, 2 * PB], "float32"),
    "fac": ("psum", [128, 6 * PB], "float32"),
}
SEMAPHORES = (["vs", "ss", "ts", "gs", "st", "ldsl", "ini", "lde0", "lde1", "ldv1", "ldv3"] + ["loc%d" % i for i in range(8)]
              + ["snap%d" % i for i in SNAPS] + ["ldb%d" % l for l in range(5)] + ["ldf%d" % l for l in range(1, 5)]
              + ["fa%d" % h for h in range(4)] + ["ba%d_%d" % (h, d) for h in range(4) for d in range(3)])


def engine_plan(src, dsts, topo, most):
    left = sorted(dsts, key=lambda c: len(topo.engines(src, c)))
    used, plan = set(), {}
    for i, c in enumerate(left):
        free = [e for e in topo.engines(src, c) if e not in used]
        share = sum(1 for x in left[i:] if set(topo.engines(src, x)) == set(topo.engines(src, c)))
        n = 1
        while 2 * n <= len(free) // share and 2 * n <= most:
            n *= 2
        plan[c] = free[:n]
        used.update(plan[c])
    return plan


def pieces(a, e):
    out = []
    while a < e:
        x = min(e, (a // K + 1) * K)
        out.append((a, x))
        a = x
    return out


def rank_program(g, core, T, topo):
    rank = T.rank_of(core)
    if rank is None:
        return
    ADD, SUB, MUL = AluOpType.add, AluOpType.subtract, AluOpType.mult
    COPY, SILU = ActivationFunctionType.Copy, ActivationFunctionType.Silu
    cores = list(T.cores)
    v = g.vector
    q = {"v": g.vector, "s": g.scalar, "t": g.tensor, "g": g, "y": g.sync}
    own = {"v": "vs", "s": "ss", "t": "ts", "g": "gs"}
    count = {"vs": 0, "ss": 0, "ts": 0, "gs": 0}
    seen = {k: {} for k in q}

    def wait(k, *tokens):
        need = {}
        for name, n in tokens:
            if n > need.get(name, 0):
                need[name] = n
        for name, n in need.items():
            if n > seen[k].get(name, 0):
                q[k].wait_ge(T.sem[name], n)
                seen[k][name] = n

    def done(k, ins):
        name = own[k]
        ins.then_inc(T.sem[name], 1)
        count[name] += 1
        return (name, count[name])

    def copy(out, in_, scale=1.0):
        return done("s", g.scalar.activation(out, in_, COPY, scale=scale))

    def calls(r, forward):
        dsts = {cores[(r + 1 + d) % N] if forward else cores[(r - 1 - d) % N]: d for d in range(3)}
        far = [c for c in dsts if topo.chip(c) != topo.chip(cores[r])]
        sets = [list(dsts)] if forward else [[c for c in dsts if c != far[-1]], far[-1:]]
        plans = [engine_plan(cores[r], x, topo, 4 if forward else WIDE) for x in sets]
        return [[(dsts[c], c, plan[c]) for c in plan] for plan in plans]

    arrive = {f: {cores[r]: len(e) for r in range(N) for call in calls(r, f) for d, c, e in call if c == core} for f in (True, False)}
    left = []

    def send(h, src, n, dst, dst_base, forward):
        name, local_each = "loc%d" % len(left), 0
        for call in calls(rank, forward):
            tr = []
            for d, c, engines in call:
                rid, pid = topo.addr(c)[:2]
                a = (h * 3 + d) * S
                sem = T.sem["fa%d" % h] if forward else T.sem["ba%d_%d" % (h, d)]
                srcs = [src[:, s * SH + d * S:s * SH + (d + 1) * S] for s in range(n)]
                tr.append(RemoteDMATransfer(dst_ids=[DstId(rid=rid, pnc=pid)], dma_engine_mask=sum(1 << e for e in engines),
                                            remote_sem=sem, srcs=srcs, dsts=[dst[:, dst_base + a:dst_base + a + S]],
                                            alu_op=1 if n > 1 else 0))
                local_each += len(engines)
            g.remote_dma_fused(tr, local_sem=T.sem[name])
        left.append((name, local_each))
        if len(left) > 1:
            lay(len(left))

    fa = {h: ("fa%d" % h, sum(arrive[True].values())) for h in range(4)}
    ba = {(h, d): ("ba%d_%d" % (h, d), arrive[False][cores[(rank + 1 + d) % N]]) for h in range(4) for d in range(3)}

    laid, k_pos, k_snap, k_list, k_free = [], {}, {}, {}, {}
    last = {"scat": []}
    late = sum(SLOTS[:7])

    def numbers(x, e):
        return T.pr[:, PAD + x:PAD + e] if x < late else T.prod[:, x - 3 * K:e - 3 * K]

    def lay(i):
        if i < len(IOTAS):
            a = sum(IOTAS[:i])
            for x, e in pieces(a, min(late, a + IOTAS[i])) + pieces(max(a, late), a + IOTAS[i]):
                laid.append((e, done("g", g.iota(numbers(x, e), [[1, e - x]], PAD + x + LIFT, 0,
                                                 allow_small_or_imprecise_dtypes=True))))

    def multiples(a, e, psum, *need):
        wait("t", k_times, *need)
        for i, src in enumerate((T.q16, T.a16, T.q16)):
            k = done("t", g.tensor.matmul(psum, T.times[:, 128 * i:128 * i + 128], src[:, a:e], i == 0, i == 2))
        return k

    def summed(i, need):
        wait("v", need)
        return done("v", v.tensor_tensor(spare[i], spare[i], T.ents[:, PARTS[i][0]:PARTS[i][1]], ADD))

    def positions(i, need):
        a, e = PARTS[i]
        wait("v", need)
        x = done("v", v.tensor_scalar(T.pos[:, a:e], spare[i], 64 * QM - 63 * AM - QM * TIMES[2], 48, ADD, MUL))
        k_pos.update({l: x for l in range(a // 192 + 1, (e - 1) // 192 + 2)})

    def scatter(i):
        a = sum(SLOTS[:i])
        for x, e in pieces(a, a + SLOTS[i]):
            l = 4 - x // K
            col = 192 * (l - 1) + (x % K) // 16
            wait("s", ("ini", 32), k_pos[l], min(t for t in laid if t[0] >= e)[1], *last["scat"])
            k = done("s", g.scalar.activation(T.inv[:, :].indirect(T.pos[:, col:col + (e - x) // 16]), numbers(x, e), SILU))
            last["scat"] = [k]
            if i < 7:
                k_free[l] = k

    def snapshot(i, *need):
        if i in SNAPS:
            h = SNAPS[i]
            wait("y", *(last["scat"] + list(need)))
            load("y", "snap%d" % i, T.invr[:, h, :, :], T.inv[0:128:16, 5 * K:6 * K])
            load("y", "snap%d" % i, T.invo[:, 192 * h:192 * h + 192], T.inv[0:128:16, h * K:(h + 1) * K])
            k_snap[h] = ("snap%d" % i, 32)
            last["scat"] = [k_snap[h]]

    def convert(h, parts=(0, 1)):
        wait("v", k_snap[h])
        for i in parts:
            out, in_ = ((T.offr[:, 40 * h:40 * h + 36], T.invr[:, h, :, 9 * h:9 * h + 9]),
                        (T.offo[:, 192 * h:192 * h + 192], T.invo[:, 192 * h:192 * h + 192]))[i]
            k_list[h, i] = done("v", v.tensor_scalar(out, in_, -LIFT, None, ADD))

    def load(k, name, out, in_):
        q[k].dma_start(out, in_).then_inc(T.sem[name], 16)

    def ld_b(l):
        load("y", "ldb%d" % l, T.bsb[:, l * M:(l + 1) * M], T.b[:, l * M:(l + 1) * M])

    def ld_v(l):
        a = K * (l - 1)
        load("y", "ldv%d" % l, T.vsb[16 * l - 16:16 * l - 8, :], T.val[:, a:a + 2 * K])

    k_v = {l: ("ldv%d" % (l - (l + 1) % 2), 16) for l in range(1, 5)}

    def ld_f(l):
        a = M if l < 4 else M + X4 if X4 < M else 2 * M + XS[3]
        a, e = K * (l - 1) + a, K * (l - 1) + (2 * M if l == 1 else K)
        for c in range(16):
            load("y", "ldf%d" % l, T.valf[c:128:16, a:e], T.val[:, a:e])

    def valf(l, a, e):
        return T.valf[:, K * (l - 1) + a:K * (l - 1) + e]

    def clear():
        wait("y", k_wz)
        load("y", "ini", T.inv[0:128:16, 0:4 * K], T.w[:, ZERO:ZERO + 4 * K // 16])
        load("y", "ini", T.inv[0:128:16, 5 * K:6 * K], T.w[:, ZERO:ZERO + K // 16])

    load("s", "ldsl", T.slr[:, :], T.sl[:, :])
    ld_b(0)
    ld_v(1)
    for i, (a, e) in enumerate(HALVES):
        load("y", "lde%d" % i, T.ents[:, a:e], T.ent[:, a:e])

    k_neg = done("v", v.memset(T.negb[:, :], -1.0))
    k_oneb = done("v", v.memset(T.oneb[:, :], 1.0))
    k_wz = done("v", v.memset(T.w[:, ZERO:ZERO + M], 0.0))
    k_first = done("g", g.iota(T.first[:, :], [[M, 4], [0, 9]], 0, 0))
    wait("g", k_neg)

    def selection(p):
        wait("g", done("g", g.affine_select(T.sel0[p:p + 8, :], T.negb[p:p + 8, :], [[1, 128]], AluOpType.is_ge, 0.0, 0, -16)))
        return done("g", g.affine_select(T.sel[p:p + 8, :], T.sel0[p:p + 8, :], [[-1, 128]], AluOpType.is_ge, 0.0, 15, 16))

    k_sel = selection(0)
    wait("g", k_oneb)
    k_idb = done("g", g.affine_select(T.idb[:, :], T.oneb[:, :], [[-1, 128]], AluOpType.is_equal, 0.0, 0, 1))
    wait("s", k_wz)
    k_pad = done("s", g.scalar.activation(T.pr[:, 0:PAD], T.w[:, ZERO:ZERO + PAD], SILU))
    start = {"clear": clear, "b1": lambda: ld_b(1), "f1": lambda: ld_f(1), "b2": lambda: ld_b(2), "f2": lambda: ld_f(2)}
    for name in LOADS[0]:
        start[name]()

    wait("v", ("ldsl", 16))
    k_sl = done("v", v.tensor_copy(T.sla[:, 0:9], T.slr[:, 0:9]))

    def sl_cols(h, d, n):
        c = h * 9 + d * 3
        return T.sla[:, c:c + n] if c % 2 == 0 else T.slb[:, c + 1:c + 1 + n]

    wait("v", k_first)
    k_slq = done("v", v.tensor_tensor(T.slq[:, :], T.slr[:, :], T.first[:, :], SUB))
    wait("v", ("ldb0", 16), k_sl)
    k_sh = done("v", v.tensor_copy(T.sh[:, 0:SH], T.bsb[:, 0:M].indirect(sl_cols(0, 0, 9))))
    wait("g", k_sh)
    send(0, T.sh, 1, T.w, R, True)
    lay(0)
    lay(1)
    wait("g", k_wz)
    k_nid = done("g", g.affine_select(T.nid[:, :], T.w[:, ZERO:ZERO + 128], [[-1, 128]], AluOpType.not_equal, -1.0, 0, 1))
    k_idf = done("g", g.affine_select(T.idf[:, :], T.w[:, ZERO:ZERO + 128], [[-1, 128]], AluOpType.not_equal, 1.0, 0, 1))
    wait("g", k_idf)
    k_sel2 = selection(32)
    wait("g", k_sel2)
    wait("y", left[0])
    for name in LOADS[1]:
        start[name]()

    if B0 == "s":
        wait("s", ("ldb0", 16))
        k_y = {0: copy(T.w[:, 0:M], T.bsb[:, 0:M])}
    else:
        k_y = {0: done("v", v.tensor_copy(T.w[:, 0:M], T.bsb[:, 0:M]))}

    wait("v", k_slq)
    done("v", v.tensor_copy(T.sla[:, 9:36], T.slq[:, 9:36]))
    k_sl = done("v", v.tensor_copy(T.slb[:, 1:37], T.slq[:, :]))
    wait("v", k_idb)
    for i, x in enumerate(TIMES):
        k_times = done("v", v.tensor_scalar(T.times[:, 128 * i:128 * i + 128], T.idb[:, :], x, None, MUL))

    banks = ((0, PB), (PB, M))
    k_bank, k_m = {}, {}

    def block_factors(e, n=M):
        return [k_bank[b] for b in range(e * M // PB, (e * M + n - 1) // PB + 1)]

    def factors(l, a, e):
        wait("t", k_sel if l < 3 else k_sel2, k_v[l])
        base, p = K * ((l - 1) % 2), 32 * (l // 3)
        while a < e:
            x = min(e, (a // PB + 1) * PB)
            k = done("t", g.tensor.matmul(T.fac[:, a:x], T.sel[p:p + 8, :], T.vsb[p:p + 8, base + a:base + x], True, True))
            k_bank[a // PB] = k
            a = x
        return k

    def shown_b(l):
        wait("s", ("ldb%d" % l, 16), k_sl)
        return copy(T.bsh[:, l * SH:(l + 1) * SH], T.bsb[:, l * M:(l + 1) * M].indirect(sl_cols(l, 0, 9)))

    def shown_v(l):
        wait("s", ("ldf%d" % l, 256), k_sl)
        return copy(T.vsh[:, l * SH:(l + 1) * SH], valf(l, M, 2 * M).indirect(sl_cols(l, 0, 9)), -1.0)

    k_f = {(l, e): ("ldf%d" % l, 256) for l in range(2, 5) for e in (1, 2, 3)}
    factors(1, 4 * PB, K)
    wait("s", k_bank[5])
    k_f[1, 3] = copy(valf(1, 4 * PB, K), T.fac[:, 4 * PB:K], -1.0)
    wait("s", factors(1, 3 * PB, 4 * PB))
    k_f[1, 2] = copy(valf(1, 3 * PB + XS[0], 4 * PB), T.fac[:, 3 * PB + XS[0]:4 * PB], -1.0)
    spare = [x[:, a:a + e - b] for (x, a), (b, e) in zip(((T.acc, 0), (T.acc, PB), (T.fac, 5 * PB)), PARTS)]

    def sixty_fourths(i):
        a, e = HALVES[i]
        wait("v", ("lde%d" % i, 16))
        return done("v", v.tensor_scalar(T.q16[:, a:e], T.ents[:, a:e], 1.0 / 64, QM - 0.5 + 0.5 / 64, MUL, ADD))

    def areas(i, need):
        a, e = HALVES[i]
        wait("v", need)
        return done("v", v.tensor_scalar(T.a16[:, a:e], T.q16[:, a:e], 1.0 / 48, AM - QM // 48 - 0.5 + 0.5 / 48, MUL, ADD))

    def places(i):
        a, e = HALVES[i]
        return done("v", v.tensor_scalar(T.offf[:, a:e], T.ents[:, a:e], 0.25, -0.375, MUL, ADD))

    x = areas(0, sixty_fourths(0))
    k_mult = [multiples(*PARTS[i], spare[i], x) for i in range(2)]
    factors(1, 0, 2 * M)
    places(0)
    x = sixty_fourths(1)
    y = summed(0, k_mult[0])
    k_round = areas(1, x)
    positions(0, y)
    y = summed(1, k_mult[1])
    k_off = places(1)
    positions(1, y)
    scatter(0)
    picks = []

    order = (3, 2, 0, 1)
    for l in range(1, 5):
        win = T.w[:, 0:R + SH * l]
        blk = [T.prod[:, e * M:(e + 1) * M] for e in range(4)]
        col = 192 * (l - 1)
        n1 = X4 if l == 4 else M
        wait("s", fa[l - 1], k_off, k_y[l - 1], *([k_m[l - 1]] if l > 1 else []))
        k_raw = {}
        n2 = XS[l - 1]
        for e, n in ((2, n2), (0, M), (1, n1)):
            if n:
                k_raw[e] = copy(T.raw[:, e * M:e * M + n], win.indirect(T.offf[:, col + 48 * e:col + 48 * e + n // 16]), -1.0 if e == 2 else 1.0)
            if (l, e) == (1, 1 if BL else 0):
                k_bsh = shown_b(1)
        if l == 1:
            k_vsh = shown_v(1)
        wait("v", fa[l - 1], k_off, k_y[l - 1], *picks)
        k_p, k_acc = {}, {}
        b_last = BL and l == 1

        def fused(e, a):
            wait("v", k_f[l, e])
            return done("v", v.tensor_tensor(T.prod[:, e * M + a:(e + 1) * M], win.indirect(T.offf[:, col + 48 * e + a // 16:col + 48 * e + 48]),
                                             valf(l, e * M + a, (e + 1) * M), MUL))

        def product(e, n):
            wait("v", k_raw[e], *block_factors(e, n))
            k_p[e] = done("v", v.tensor_tensor(T.prod[:, e * M:e * M + n], T.raw[:, e * M:e * M + n], T.fac[:, e * M:e * M + n], MUL))

        def shown(out, window, other, op, *need):
            wait("v", k_sl, *need)
            return done("v", v.tensor_tensor(out, window.indirect(sl_cols(l, 0, 9)), other, op))

        def tensor_add(j, i):
            a, e = banks[j]
            wait("t", k_two if (i, j) == (1, 1) else k_p[order[i]], k_nid)
            k_acc[j] = done("t", g.tensor.matmul(T.acc[:, a:e], T.nid[:, :], T.prod[:, order[i] * M + a:order[i] * M + e],
                                                 b_last and i == 0, not b_last and i == TA[l - 1][j] - 1))

        def vector_add(i):
            for j in sorted(range(2), key=lambda j: TA[l - 1][j]):
                a, e = banks[j]
                if i >= TA[l - 1][j]:
                    wait("v", k_p[order[i]], k_acc[j])
                    out = T.acc[:, a:e] if i < 3 else T.w[:, l * M + a:l * M + e]
                    k_y[l] = k_acc[j] = done("v", v.tensor_tensor(out, T.acc[:, a:e], T.prod[:, order[i] * M + a:order[i] * M + e],
                                                                  SUB if i < 2 or (i == 3 and a >= n1) else ADD))

        k_p[3] = fused(3, 0)
        k_p[2] = k_two = fused(2, n2)
        if n2:
            product(2, n2)
        wait("t", k_y[l - 1], k_idb, *k_pos.values())

        def with_b(j, first):
            a, e = banks[j]
            wait("t", ("ldb%d" % l, 16))
            k_acc[j] = done("t", g.tensor.matmul(T.acc[:, a:e], T.idb[:, :], T.bsb[:, l * M + a:l * M + e], first, not first))

        if not b_last:
            with_b(0, True)
            with_b(1, True)
        for i in range(2):
            for j in sorted(range(2), key=lambda j: TA[l - 1][j]):
                if i < TA[l - 1][j]:
                    tensor_add(j, i)
                    if b_last and i == TA[l - 1][j] - 1:
                        with_b(j, False)
        if l < 4:
            mine = slice(l * SH, (l + 1) * SH)
            picks = []
            for i in range(NS):
                wait("s", k_p[3 - i], left[-1])
                picks.append(copy(T.sh[:, (2 + i) * SH:(3 + i) * SH], blk[3 - i].indirect(sl_cols(l, 0, 9)), -1.0))
            x, part = k_bsh, T.bsh[:, mine]
            if b_last:
                product(0, M)
            if NS == 0:
                x, part = shown(T.c0[:, :], blk[3], part, SUB, k_p[3], x), T.c0[:, :]
            if not b_last:
                product(0, M)
            if NS < 2:
                x, part = shown(T.c1[:, :], blk[2], part, SUB if NS else ADD, k_p[2], x), T.c1[:, :]
            shown(T.sh[:, SH:2 * SH], T.raw[:, M:2 * M], T.vsh[:, mine], MUL, k_raw[1], k_vsh, left[-1])
            wait("g", shown(T.sh[:, 0:SH], blk[0], part, SUB if NS < 2 else ADD, k_p[0], x), *picks)
            send(l, T.sh, 2 + NS, T.w, R, True)
        else:
            factors(4, 4 * PB if n2 else 3 * PB, K)
            if n1 < M:
                fused(1, n1)
            product(0, M)
        snapshot(l - 1, fa[l - 1])
        vector_add(1)
        product(1, n1)
        k_m[l] = k_p[1]
        if l < 4:
            wait("y", left[l])
            if l == 1:
                ld_v(3)
            if l < 3:
                ld_b(l + 2)
                ld_f(l + 2)
        scatter(l)
        if l == 3:
            wait("v", ("ini", 32))
        vector_add(2)
        if l == LATE + 1:
            k_sum = summed(2, k_mult)
        vector_add(3)
        if l == LATE + 1:
            positions(2, k_sum)
        if l < 4:
            wait("t", k_f[1, 2])
            if l == LATE:
                k_mult = multiples(*PARTS[2], spare[2], k_round)
            wait("t", k_m[l])
            if XS[l]:
                factors(l + 1, 2 * M, 4 * PB if l == 3 else 2 * M + XS[l])
            factors(l + 1, 0, 2 * M)
            if l < 3:
                k_bsh, k_vsh = shown_b(l + 1), shown_v(l + 1)
            if l == 3:
                convert(3)

    def start_acc(l, need):
        wait("t", need, k_idf)
        bank = PB * (l % 2)
        done("t", g.tensor.matmul(T.acc[:, bank:bank + M - VAS[l]], T.idf[:, :], T.w[:, l * M + VAS[l]:(l + 1) * M], True, False))

    k_z = k_y[4]
    start_acc(3, k_z)
    for l in range(4, -1, -1):
        if l < 4:
            VA = VAS[l]
            SB = M - VA
            win = T.pr[:, 0:PAD + K * (4 - l)]
            wl = T.w[:, M * l:M * (l + 1)]
            acc = T.acc[:, PB * (l % 2):PB * (l % 2) + SB]
            wait("s", k_pr, k_list[l, 0], k_pad, left[-1])
            wait("v", k_pr, k_list[l, 0], k_pad)

            def raw_slot(s):
                wait("s", k_list[l, 1])
                return copy(T.raw[:, s * SB:(s + 1) * SB] if s < 3 else T.prod[:, XA + VA:XA + M],
                            win.indirect(T.offo[:, 192 * l + 48 * s + VA // 16:192 * l + 48 * (s + 1)]))

            k_raw = [raw_slot(s) for s in range(RF[l])]
            if TAIL[l] == 0:
                wait("g", copy(T.rsum[:, :], win.indirect(T.offr[:, 40 * l:40 * l + 36])))
                send(l, T.rsum, 4, T.rc, 0, False)
            else:
                lo, hi = (win.indirect(T.offr[:, 40 * l + c:40 * l + c + 18]) for c in (0, 18))
                wait("v", left[-1])
                if TAIL[l] == 3:
                    wait("g", copy(T.rsum[:, 0:2 * SH], lo), done("v", v.tensor_copy(T.rsum[:, 2 * SH:4 * SH], hi)))
                    send(l, T.rsum, 4, T.rc, 0, False)
                else:
                    wait("v", done("v", v.tensor_copy(T.rsum[:, 2 * SH:4 * SH], lo)) if TAIL[l] == 1 else copy(T.rsum[:, 2 * SH:4 * SH], lo))
                    wait("g", done("v", v.tensor_tensor(T.rsum[:, 0:2 * SH], hi, T.rsum[:, 2 * SH:4 * SH], ADD)))
                    send(l, T.rsum, 2, T.rc, 0, False)
            k_raw += [raw_slot(s) for s in range(RF[l], 4)]
            if l > 0:
                snapshot(7 - l)
            early = set(k_snap)
            wait("t", k_pr)
            if l > 0:
                factors(l, 0, FB[l] * PB)
            for s in range(3):
                wait("t", k_raw[s])
                k_t = done("t", g.tensor.matmul(acc, T.idf[:, :], T.raw[:, s * SB:(s + 1) * SB], False, s == 2))
            if l > 0:
                factors(l, FB[l] * PB, 5 * PB)
            wait("v", k_list[l, 1])
            cut = VA // 64 * 32
            parts = ((0, cut), (cut, VA))
            k_h = [k_z, k_z]

            def own_slot(s):
                for h, (a, e) in enumerate(parts):
                    wait("v", k_h[h])
                    at = [M * l, 0, VA, XA, M * l]
                    src = (T.w if s == 0 else T.prod)[:, at[s] + a:at[s] + e]
                    out = (T.w if s == 3 else T.prod)[:, at[s + 1] + a:at[s + 1] + e]
                    c = 192 * l + 48 * s
                    k_h[h] = done("v", v.tensor_tensor(out, win.indirect(T.offo[:, c + a // 16:c + e // 16]), src, ADD))

            for s in range(3):
                own_slot(s)
            if l > 0:
                scatter(8 - l)
            if l == 1:
                snapshot(7)
            fill = [lambda: convert(l - 1, (0,)), lambda: convert(l - 1, (1,))] if l - 1 in early else []

            def arrival(d, *need):
                a = (l * 3 + d) * S
                wait("v", *need)
                x = done("v", v.tensor_copy(T.tmp[:, :], wl.indirect(sl_cols(l, d, 3))))
                if fill:
                    fill.pop(0)()
                wait("v", x, ba[l, d])
                return done("v", v.tensor_tensor(wl.indirect(sl_cols(l, d, 3)), T.tmp[:, :], T.rc[:, a:a + S], ADD))

            ds = sorted(range(3), key=lambda d: topo.chip(cores[(rank + 1 + d) % N]) != topo.chip(core))
            own_slot(3)
            wait("v", k_t, k_raw[3])
            k_z = done("v", v.tensor_tensor(T.w[:, M * l + VA:M * (l + 1)], acc, T.prod[:, XA + VA:XA + M], ADD))
            if fill:
                fill.pop()()
            if l > 0:
                factors(l, 5 * PB, K)
                start_acc(l - 1, k_h[0])
            for d in ds:
                k_z = arrival(d, k_z)
        zl = T.w[:, l * M:(l + 1) * M]
        wait("y", k_z)
        load("y", "st", T.z[:, l * M:(l + 1) * M], zl)
        if l > 0:
            wait("v", k_z, k_free[l])
            base = PAD + K * (4 - l)
            for e in range(4):
                wait("v", *block_factors(e))
                if e == 3 and (l - 1, 0) not in k_list and not CL:
                    convert(l - 1)
                k_pr = done("v", v.tensor_tensor(T.pr[:, base + e * M:base + (e + 1) * M], zl, T.fac[:, e * M:(e + 1) * M], MUL))
            if (l - 1, 0) not in k_list:
                convert(l - 1)
    wait("y", ("st", 80))
    wait("g", *left)
    wait("v", ("ss", count["ss"]), ("ts", count["ts"]), ("gs", count["gs"]))
